import numpy as np
import ml_dtypes


def mxq(x, axis, fmt="e4m3"):
    dtype, down = {"e4m3": (ml_dtypes.float8_e4m3fn, 7), "e5m2": (ml_dtypes.float8_e5m2, 14)}[fmt]
    v = np.moveaxis(np.asarray(x, np.float32).astype(ml_dtypes.bfloat16).astype(np.float64), axis, -1)
    blocks = v.reshape(v.shape[:-1] + (-1, 32))
    amax = np.abs(blocks).max(-1, keepdims=True)
    byte = np.maximum(np.where(amax > 0, np.frexp(amax)[1] - 1 + 127, 0) - down, 1)
    scale = np.exp2(byte - 127.0)
    codes = (blocks / scale).astype(np.float32).astype(dtype).astype(np.float64)
    return np.moveaxis((codes * scale).reshape(v.shape), -1, axis)


WIDE = False


def mx_kscale(k):
    if not WIDE:
        return np.ones(k)
    levels = np.array([10, -10, 5, -5, 0])
    if k % 512:
        return np.exp2(np.random.permutation(np.resize(levels, k // 32))).repeat(32)
    a = np.empty((k // 512, 16))
    for p in range(k // 512):
        a[p, :8] = np.random.permutation(np.resize(levels, 8))
        for g in range(8):
            far = levels[np.abs(levels - a[p, g]) >= 10]
            a[p, g + 8] = far[np.random.randint(len(far))]
    return np.exp2(a.ravel()).repeat(32)


def f64(x):
    return np.asarray(x).astype(np.float64)


def striped(idx):
    return np.tile(idx.reshape(-1, 16).T, (8, 1)).astype(np.uint16)


def unstriped(offs):
    return offs[:16].T.reshape(-1).astype(np.int64)


E2M1 = np.array([0.0, 0.5, 1.0, 1.5, 2.0, 3.0, 4.0, 6.0, -0.0, -0.5, -1.0, -1.5, -2.0, -3.0, -4.0, -6.0])


def pack_weight(w, fmt):
    k, n = w.shape
    w = f64(np.asarray(w, np.float32).astype(ml_dtypes.bfloat16)).reshape(k // 32, 32, n)
    amax = np.abs(w).max(1)
    if fmt == "e4m3":
        byte = np.frexp(amax)[1] - 1 + 127 - 7
    else:
        mant, ex = np.frexp(amax / 6.0)
        byte = np.where(mant > 0.5, ex, ex - 1) + 127
    byte = np.clip(np.where(amax > 0, byte, 1), 1, 254)
    scaled = (w * np.exp2(127.0 - byte)[:, None, :]).reshape(k, n).astype(np.float32)
    by_word = np.ascontiguousarray(scaled.reshape(k // 512, 128, 4, n).transpose(0, 1, 3, 2))
    if fmt == "e4m3":
        words = by_word.astype(ml_dtypes.float8_e4m3fn).view(np.uint8)
    else:
        c = by_word.astype(ml_dtypes.float4_e2m1fn).view(np.uint8) & 0xF
        words = (c[..., 0::2] | (c[..., 1::2] << 4)).reshape(k // 512, 128, 2 * n)
    return np.ascontiguousarray(words), np.ascontiguousarray(byte.astype(np.uint8).reshape(k // 512, 16, n))


def unpack_weight(words, scales, fmt):
    g, _, n = scales.shape
    words = np.ascontiguousarray(words).reshape(g, 128, n, -1)
    if fmt == "e4m3":
        vals = words.view(ml_dtypes.float8_e4m3fn).astype(np.float64)
    else:
        nib = np.empty((g, 128, n, 4), np.uint8)
        nib[..., 0::2] = words & 0xF
        nib[..., 1::2] = words >> 4
        vals = E2M1[nib]
    vals = vals * np.repeat(np.exp2(scales.astype(np.float64) - 127.0), 8, axis=1)[..., None]
    return vals.transpose(0, 1, 3, 2).reshape(g * 512, n)


def gelu(v):
    return 0.5 * v * (1.0 + np.tanh(np.sqrt(2.0 / np.pi) * (v + 0.044715 * v**3)))


K, K2, T, T3, S, P, H, N = 1024, 512, 4096, 2048, 1024, 512, 1024, 512

def setup_inputs():
    n = np.random.standard_normal
    s, s2, u = mx_kscale(K)[:, None], mx_kscale(K2)[:, None], mx_kscale(H)[:, None]
    d = {}
    d["tab_words"], d["tab_scales"] = pack_weight(n((K, T)) * s, "e4m3")
    d["tab2_words"], d["tab2_scales"] = pack_weight(n((K2, T3)) * s2, "e4m3")
    d["offs"] = striped(np.random.permutation(T)[:S])
    d["offs2"] = striped(np.random.permutation(T3)[:P])
    d["pos1"] = striped(np.random.permutation(S)[:P])
    d["w1_words"], d["w1_scales"] = pack_weight(1.8 * n((K, H)) / K ** 0.5 / s, "e2m1")
    d["w2"] = (1.3 * n((K2, H)) / K2 ** 0.5 / s2 * u.T).astype(np.float32)
    d["w3_words"], d["w3_scales"] = pack_weight(n((H, N)) / H ** 0.5 / u, "e4m3")
    d["gain"] = (np.exp(0.3 * n(H)) * u[:, 0]).astype(np.float32)
    d["cap"] = ((0.3 + n((H, P))) * u).astype(np.float32)
    d["wgs"] = np.exp(0.3 * n((128, P))).astype(np.float32)
    d["place"] = (1.2 * n((H, S))).astype(np.float32)
    return d

def reference(tab_words, tab_scales, tab2_words, tab2_scales, offs, offs2, pos1, w1_words, w1_scales, w2, w3_words, w3_scales, gain, cap, wgs, place):
    v = unpack_weight(tab_words, tab_scales, "e4m3")[:, unstriped(offs)]
    v2 = unpack_weight(tab2_words, tab2_scales, "e4m3")[:, unstriped(offs2)]
    w1 = unpack_weight(w1_words, w1_scales, "e2m1")
    w3 = unpack_weight(w3_words, w3_scales, "e4m3")
    rough = w1.T @ v
    a = f64(gain)[:, None] * np.sqrt(1.0 + np.square(rough))
    b = np.minimum(mxq(f64(w2), 0, "e4m3").T @ v2, f64(cap))
    placed = np.zeros((H, S))
    placed[:, unstriped(pos1)] = np.tile(f64(wgs), (H // 128, 1)) * b
    z = a + placed * f64(place)
    y = w3.T @ mxq(z, 0, "e4m3")
    return np.log(1.0 + np.abs(y))

@@ -1,0 +1,261 @@
+from contextlib import ExitStack
+
+import concourse.mybir as mybir
+from concourse.masks import make_identity
+
+K, K2, T, T3, S, P2, H, N = 1024, 512, 4096, 2048, 1024, 512, 1024, 512
+FLOPS = 2 * (K * H * S + K2 * H * P2 + H * N * S)
+
+F32 = mybir.dt.float32
+BF16 = mybir.dt.bfloat16
+I32 = mybir.dt.int32
+U32 = mybir.dt.uint32
+U16 = mybir.dt.uint16
+U8 = mybir.dt.uint8
+FP8X4 = mybir.dt.float8_e4m3fn_x4
+FP4X4 = mybir.dt.float4_e2m1fn_x4
+ACT = mybir.ActivationFunctionType
+ALU = mybir.AluOpType
+
+P = 128
+BANK = 512
+HALF = S // 2
+CHUNKS = [(0, 256), (256, 256), (512, 256), (768, 128), (896, 128)]
+RUN = 4
+
+
+def tile_list_hull_drag_features_kernel(tc, tab_words, tab_scales, tab2_words, tab2_scales, offs, offs2, pos1,
+                                                 w1_words, w1_scales, w2, w3_words, w3_scales, gain, cap, wgs, place, out):
+    nc = tc.nc
+    with ExitStack() as ctx:
+        lists = ctx.enter_context(tc.tile_pool(name="lists", bufs=1))
+        keep = ctx.enter_context(tc.tile_pool(name="keep", bufs=1))
+        shared = ctx.enter_context(tc.tile_pool(name="shared", bufs=1))
+        ring = ctx.enter_context(tc.tile_pool(name="ring", bufs=2))
+        psum = ctx.enter_context(tc.psum_pool(name="psum", bufs=2))
+
+        idx = lists.tile([P, S // 16], U16, name="idx")
+        idx2 = lists.tile([P, P2 // 16], U16, name="idx2")
+        p1 = lists.tile([P, P2 // 16], U16, name="p1")
+
+        tab2_w = shared.tile([P, T3], I32, name="tab2_w", offset=8 * T)
+        tab2_s = keep.tile([P, T3], U8, name="tab2_s", align_bytes=64)
+        tab_s = keep.tile([P, T], U8, name="tab_s", align_bytes=64)
+        tab_w = [shared.tile([P, T], I32, name=f"tab_w{a}", offset=4 * T * a) for a in range(2)]
+        v2_w = keep.tile([P, P2], U32, name="v2_w", align_bytes=64)
+        v2_s = keep.tile([P, P2], U8, name="v2_s", align_bytes=64)
+        v_w = [keep.tile([P, S], U32, name=f"v_w{a}", align_bytes=64) for a in range(2)]
+        v_s = [keep.tile([P, S], U8, name=f"v_s{a}", align_bytes=64) for a in range(2)]
+        w1_w = keep.tile([P, 2, 2 * H], U8, name="w1_w", align_bytes=64)
+        w1_s = keep.tile([P, 2, H], U8, name="w1_s", align_bytes=64)
+        w3_w = keep.tile([P, 2, N], I32, name="w3_w", align_bytes=64)
+        w3_s = keep.tile([P, 2, N], U8, name="w3_s", align_bytes=64)
+        w2_raw = [keep.tile([P, 4, BANK], F32, name="w2_raw0"), shared.tile([P, 4, BANK], F32, name="w2_raw1", offset=8 * T + 4 * T3)]
+        gain_sb = keep.tile([P, 2, 4], F32, name="gain_sb")
+        wgs_sb = [keep.tile([P, 2, P2], F32, name=f"wgs{u}") for u in range(2)]
+        cap_sb = {(b, u): ring.tile([P, 2, P2], F32, name=f"cap{b}{u}", tag="cap_out", bufs=4) for b in range(2) for u in range(2)}
+        place_sb = {(h, b): keep.tile([P, 4, HALF], F32, name=f"place{h}{b}") for h in range(2) for b in range(2)}
+        pages = {(0, t): keep.tile([P, S], F32, name=f"page0{t}") for t in range(4)}
+        ident = keep.tile([P, P], F32, name="ident")
+
+        for tile_s in (tab2_s, tab_s):
+            nc.gpsimd.memset(tile_s[:].bitcast(I32), 0)
+        for tile_s in (w1_s, w3_s, v_s[1]):
+            nc.vector.memset(tile_s[:].bitcast(I32), 0)
+        for page in pages.values():
+            nc.vector.memset(page[:], 0.0)
+        make_identity(nc, ident[:])
+
+        def load_scales(tile_s, dram):
+            rows = dram.bitcast(I32).rearrange("a (q r) c -> q r a c", r=4)
+            for q in range(4):
+                nc.sync.dma_start(out=tile_s[32 * q : 32 * q + 4].bitcast(I32), in_=rows[q])
+
+        def load_w2(b):
+            nc.sync.dma_start(out=w2_raw[b][:], in_=w2.rearrange("(p j) c -> p j c", j=4)[:, :, BANK * b : BANK * (b + 1)])
+
+        def load_cap(b, u):
+            rows = cap[BANK * b : BANK * (b + 1), :].rearrange("(p t) j -> p t j", t=4)
+            nc.sync.dma_start(out=cap_sb[b, u][:], in_=rows[:, 2 * u : 2 * u + 2, :])
+
+        def load_wgs(u):
+            rows = wgs.rearrange("(p t) j -> p t j", t=4)[:, 2 * u : 2 * u + 2, :]
+            for q in range(4):
+                nc.sync.dma_start(out=wgs_sb[u][32 * q : 32 * (q + 1)], in_=rows)
+
+        def load_tab(a):
+            nc.sync.dma_start(out=tab_w[a][:], in_=tab_words[a].rearrange("p t i -> p (t i)").bitcast(I32))
+
+        nc.sync.dma_start(idx2[:], offs2)
+        nc.sync.dma_start(out=tab2_w[:], in_=tab2_words[0].rearrange("p t i -> p (t i)").bitcast(I32))
+        for q in range(4):
+            nc.sync.dma_start(out=tab2_s[32 * q : 32 * q + 4, :].bitcast(I32), in_=tab2_scales[0, 4 * q : 4 * q + 4, :].bitcast(I32))
+        load_w2(0)
+        nc.sync.dma_start(p1[:], pos1)
+        load_cap(0, 0)
+        load_wgs(0)
+        nc.sync.dma_start(idx[:], offs)
+        for q in range(4):
+            nc.sync.dma_start(out=tab_s[32 * q : 32 * q + 8, :].bitcast(I32), in_=tab_scales[:, 4 * q : 4 * q + 4, :].bitcast(I32))
+        load_w2(1)
+        load_tab(0)
+        load_scales(w1_s, w1_scales)
+        nc.sync.dma_start(out=w1_w[:].bitcast(I32), in_=w1_words.bitcast(I32).rearrange("a p c -> p a c"))
+        load_tab(1)
+        nc.sync.dma_start(out=gain_sb[:], in_=gain.rearrange("(b p t) -> p b t", b=2, t=4))
+        load_cap(0, 1)
+        load_wgs(1)
+        load_cap(1, 0)
+        load_cap(1, 1)
+        load_scales(w3_s, w3_scales)
+        nc.sync.dma_start(out=w3_w[:], in_=w3_words.rearrange("a p c i -> p a (c i)").bitcast(I32))
+        for h in range(2):
+            for b in range(2):
+                rows = place[BANK * b : BANK * (b + 1), :].rearrange("(p t) j -> p t j", t=4)
+                nc.sync.dma_start(out=place_sb[h, b][:], in_=rows[:, :, HALF * h : HALF * (h + 1)])
+
+        nc.vector.tensor_copy(v2_w[:], tab2_w[:].bitcast(U32).indirect(idx2[:]))
+        nc.vector.tensor_copy(v2_s[:], tab2_s[:].indirect(idx2[:]))
+
+        w2_q = {}
+
+        def quantise_w2(b, u, on_vector):
+            grouped = ring.tile([P, 2, P, 4], BF16, name="w2_grouped", align_bytes=64, bufs=4)
+            src = w2_raw[b][:].rearrange("p j (m t) -> p m j t", t=4)[:, :, :, 2 * u : 2 * u + 2]
+            dst = grouped[:].rearrange("p t m j -> p m j t")
+            if on_vector:
+                nc.vector.tensor_copy(out=dst, in_=src)
+            else:
+                nc.scalar.copy(out=dst, in_=src)
+            codes = keep.tile([P, 2 * P], U32, name=f"w2_codes{b}{u}", align_bytes=64)
+            scales = keep.tile([P, 2 * P], U8, name=f"w2_scales{b}{u}", align_bytes=64)
+            nc.vector.quantize_mx(out=codes[:].bitcast(FP8X4), scales=scales[:], in_=grouped[:].rearrange("p t m j -> p (t m j)"))
+            w2_q[b, u] = (codes, scales)
+
+        limited = {}
+
+        def limit(b, t):
+            codes, scales = w2_q[b, t // 2]
+            cols = slice(P * (t % 2), P * (t % 2 + 1))
+            acc = psum.tile([P, BANK], F32, name="acc_b", tag="acc_by", bufs=4)
+            nc.tensor.matmul_mx(out=acc[:], lhsT=codes[:, cols].bitcast(FP8X4), lhsT_scale=scales[:, cols],
+                                rhs=v2_w[:].bitcast(FP8X4), rhs_scale=v2_s[:], start=True, stop=True)
+            low = ring.tile([P, P2], F32, name="low", bufs=3)
+            nc.vector.tensor_tensor(out=low[:], in0=acc[:], in1=cap_sb[b, t // 2][:, t % 2, :], op=ALU.min)
+            limited[b, t] = low
+
+        def put(b, t):
+            nc.vector.tensor_tensor(pages[b, t][:].indirect(p1[:]), limited[b, t][:], wgs_sb[t // 2][:, t % 2, :], ALU.mult)
+
+        quantise_w2(0, 0, True)
+        quantise_w2(0, 1, False)
+        limit(0, 0)
+        limit(0, 1)
+        put(0, 0)
+        put(0, 1)
+
+        nc.vector.tensor_copy(v_s[0][:], tab_s[:].indirect(idx[:]))
+        for q in range(4):
+            nc.scalar.dma_start(out=v_s[1][32 * q : 32 * q + 4, :].bitcast(I32), in_=v_s[0][32 * q + 4 : 32 * q + 8, :].bitcast(I32))
+        quantise_w2(1, 0, False)
+        quantise_w2(1, 1, False)
+        for t in range(4):
+            pages[1, t] = shared.tile([P, S], F32, name=f"page1{t}", offset=8 * T + 4 * S * t)
+            nc.gpsimd.memset(pages[1, t][:], 0.0)
+        nc.vector.tensor_copy(v_w[0][:], tab_w[0][:].bitcast(U32).indirect(idx[:]))
+        for h in range(2):
+            nc.vector.tensor_copy(v_w[1][:, HALF * h : HALF * (h + 1)],
+                                  tab_w[1][:].bitcast(U32).indirect(idx[:, HALF // 16 * h : HALF // 16 * (h + 1)]))
+
+        slices = [(0, 2), (0, 3), (1, 0), (1, 1), (1, 2), (1, 3)]
+        limit(*slices[0])
+        for now, ahead in zip(slices, slices[1:] + [None]):
+            if ahead is not None:
+                limit(*ahead)
+            put(*now)
+
+        a_sb = {}
+        roots = {}
+
+        def square(h, b, jt):
+            if jt == 0:
+                roots[h, b] = ring.tile([P, 4, BANK], F32, name="root")
+            cols = slice(HALF * h + P * jt, HALF * h + P * (jt + 1))
+            acc = psum.tile([P, BANK], F32, name="acc_rough")
+            for a in range(2):
+                nc.tensor.matmul_mx(out=acc[:], lhsT=v_w[a][:, cols].bitcast(FP8X4), lhsT_scale=v_s[a][:, cols],
+                                    rhs=w1_w[:, a, 2 * BANK * b : 2 * BANK * (b + 1)].bitcast(FP4X4),
+                                    rhs_scale=w1_s[:, a, BANK * b : BANK * (b + 1)], start=(a == 0), stop=(a == 1))
+            nc.scalar.activation(out=roots[h, b][:, jt, :].rearrange("p (t q) -> p t q", t=4),
+                                 in_=acc[:].rearrange("p (q t) -> p t q", t=4), func=ACT.Square)
+
+        def root(h, b):
+            whole = roots[h, b][:].rearrange("p jt c -> p (jt c)")
+            nc.scalar.activation(out=whole, in_=whole, func=ACT.Sqrt, bias=1.0)
+
+        def turn(h, b, t):
+            if t == 0:
+                a_sb[h, b] = shared.tile([P, 4, HALF], F32, name=f"a{h}{b}", offset=4 * 4 * HALF * (2 * h + b))
+            turned = psum.tile([P, BANK], F32, name="turned")
+            for jt in range(4):
+                nc.tensor.transpose(turned[:, P * jt : P * (jt + 1)], roots[h, b][:, jt, P * t : P * (t + 1)], ident[:])
+            nc.scalar.activation(out=a_sb[h, b][:, t, :], in_=turned[:], func=ACT.Copy, scale=gain_sb[:, b, t : t + 1])
+
+        units = [(h, b) for h in range(2) for b in range(2)]
+        for before, now in zip([None] + units, units + [None]):
+            for pair in range(2):
+                for x in (2 * pair, 2 * pair + 1):
+                    if now is not None:
+                        square(*now, x)
+                for x in (2 * pair, 2 * pair + 1):
+                    if before is not None:
+                        turn(*before, x)
+            if now is not None:
+                root(*now)
+
+        z_bf = {}
+        scaled = {}
+        all_rows = [(b, t) for b in range(2) for t in range(4)]
+
+        def scale_by_place(c0, w, rows):
+            h, local = c0 // HALF, slice(c0 % HALF, c0 % HALF + w)
+            if c0 not in scaled:
+                scaled[c0] = ring.tile([P, 2, 4, w], F32, name="scaled")
+            for b, t in rows:
+                nc.vector.tensor_tensor(out=scaled[c0][:, b, t, :], in0=pages[b, t][:, c0 : c0 + w], in1=place_sb[h, b][:, t, local], op=ALU.mult)
+
+        def add_up(c0, w):
+            h, local = c0 // HALF, slice(c0 % HALF, c0 % HALF + w)
+            z = ring.tile([P, 2, w, 4], BF16, name="z_bf", align_bytes=64)
+            for b in range(2):
+                nc.vector.tensor_tensor(out=z[:, b].rearrange("p (c i) t -> p c t i", i=RUN),
+                                        in0=a_sb[h, b][:, :, local].rearrange("p t (c i) -> p c t i", i=RUN),
+                                        in1=scaled[c0][:, b].rearrange("p t (c i) -> p c t i", i=RUN), op=ALU.add)
+            z_bf[c0] = z
+
+        def finish(c0, w):
+            codes = ring.tile([P, 2 * w], U32, name="z_codes", align_bytes=64)
+            scales = ring.tile([P, 2 * w], U8, name="z_scales", align_bytes=64)
+            nc.vector.quantize_mx(out=codes[:].bitcast(FP8X4), scales=scales[:], in_=z_bf[c0][:].rearrange("p b c t -> p (b c t)"))
+            res = ring.tile([P, 4 * w], F32, name="res", tag="cap_out", bufs=4)
+            per_bank = BANK // w
+            for first in range(0, 4, per_bank):
+                acc = psum.tile([P, BANK], F32, name="acc_y", tag="acc_by", bufs=4)
+                for g in range(per_bank):
+                    cols = slice(P * (first + g), P * (first + g + 1))
+                    for b in range(2):
+                        nc.tensor.matmul_mx(out=acc[:, w * g : w * (g + 1)], lhsT=w3_w[:, b, cols].bitcast(FP8X4), lhsT_scale=w3_s[:, b, cols],
+                                            rhs=codes[:, w * b : w * (b + 1)].bitcast(FP8X4), rhs_scale=scales[:, w * b : w * (b + 1)],
+                                            start=(b == 0), stop=(b == 1))
+                nc.scalar.activation(out=res[:, w * first : w * first + BANK], in_=acc[:], func=ACT.Abs)
+            nc.scalar.activation(out=res[:], in_=res[:], func=ACT.Ln, bias=1.0)
+            nc.sync.dma_start(out=out.rearrange("(g p) j -> p g j", p=P)[:, :, c0 : c0 + w], in_=res[:].rearrange("p (g j) -> p g j", g=4))
+
+        for before, now in zip([None] + CHUNKS, CHUNKS + [None]):
+            if now is not None:
+                scale_by_place(*now, all_rows[:1])
+            if before is not None:
+                finish(*before)
+            if now is not None:
+                scale_by_place(*now, all_rows[1:])
+                add_up(*now)

@@ -1,7 +1,6 @@
 from contextlib import ExitStack
 
 import concourse.mybir as mybir
-from concourse.masks import make_identity
 
 K, K2, T, T3, S, P2, H, N = 1024, 512, 4096, 2048, 1024, 512, 1024, 512
 FLOPS = 2 * (K * H * S + K2 * H * P2 + H * N * S)
@@ -22,6 +21,8 @@ BANK = 512
 HALF = S // 2
 CHUNKS = [(0, 256), (256, 256), (512, 256), (768, 128), (896, 128)]
 RUN = 4
+CAP_LOADS = [(0, 2), (2, 2), (4, 1), (5, 1), (6, 1), (7, 1)]
+A_OFFSETS = [0, 2 * T, 4 * T, 8 * T]
 
 
 def tile_list_hull_drag_features_kernel(tc, tab_words, tab_scales, tab2_words, tab2_scales, offs, offs2, pos1,
@@ -50,21 +51,17 @@ def tile_list_hull_drag_features_kernel(tc, tab_words, tab_scales, tab2_words, t
         w1_s = keep.tile([P, 2, H], U8, name="w1_s", align_bytes=64)
         w3_w = keep.tile([P, 2, N], I32, name="w3_w", align_bytes=64)
         w3_s = keep.tile([P, 2, N], U8, name="w3_s", align_bytes=64)
-        w2_raw = [keep.tile([P, 4, BANK], F32, name="w2_raw0"), shared.tile([P, 4, BANK], F32, name="w2_raw1", offset=8 * T + 4 * T3)]
+        w2_raw = [shared.tile([P, 4, BANK], F32, name="w2_raw0", offset=10 * T), keep.tile([P, 4, BANK], F32, name="w2_raw1")]
         gain_sb = keep.tile([P, 2, 4], F32, name="gain_sb")
         wgs_sb = [keep.tile([P, 2, P2], F32, name=f"wgs{u}") for u in range(2)]
-        cap_sb = {(b, u): ring.tile([P, 2, P2], F32, name=f"cap{b}{u}", tag="cap_out", bufs=4) for b in range(2) for u in range(2)}
-        place_sb = {(h, b): keep.tile([P, 4, HALF], F32, name=f"place{h}{b}") for h in range(2) for b in range(2)}
-        pages = {(0, t): keep.tile([P, S], F32, name=f"page0{t}") for t in range(4)}
-        ident = keep.tile([P, P], F32, name="ident")
+        cap_sb = {first: ring.tile([P, count, P2], F32, name=f"cap{first}", tag="cap_out", bufs=6) for first, count in CAP_LOADS}
+        place_sb = [keep.tile([P, 4, S], F32, name=f"place{b}") for b in range(2)]
+        pages = [keep.tile([P, S], F32, name="page0")]
 
-        for tile_s in (tab2_s, tab_s):
-            nc.gpsimd.memset(tile_s[:].bitcast(I32), 0)
-        for tile_s in (w1_s, w3_s, v_s[1]):
+        nc.gpsimd.memset(tab2_s[:].bitcast(I32), 0)
+        for tile_s in (w1_s, tab_s, w3_s, v_s[1]):
             nc.vector.memset(tile_s[:].bitcast(I32), 0)
-        for page in pages.values():
-            nc.vector.memset(page[:], 0.0)
-        make_identity(nc, ident[:])
+        nc.vector.memset(pages[0][:], 0.0)
 
         def load_scales(tile_s, dram):
             rows = dram.bitcast(I32).rearrange("a (q r) c -> q r a c", r=4)
@@ -74,9 +71,10 @@ def tile_list_hull_drag_features_kernel(tc, tab_words, tab_scales, tab2_words, t
         def load_w2(b):
             nc.sync.dma_start(out=w2_raw[b][:], in_=w2.rearrange("(p j) c -> p j c", j=4)[:, :, BANK * b : BANK * (b + 1)])
 
-        def load_cap(b, u):
+        def load_cap(first):
+            b, t = divmod(first, 4)
             rows = cap[BANK * b : BANK * (b + 1), :].rearrange("(p t) j -> p t j", t=4)
-            nc.sync.dma_start(out=cap_sb[b, u][:], in_=rows[:, 2 * u : 2 * u + 2, :])
+            nc.sync.dma_start(out=cap_sb[first][:], in_=rows[:, t : t + dict(CAP_LOADS)[first], :])
 
         def load_wgs(u):
             rows = wgs.rearrange("(p t) j -> p t j", t=4)[:, 2 * u : 2 * u + 2, :]
@@ -86,36 +84,39 @@ def tile_list_hull_drag_features_kernel(tc, tab_words, tab_scales, tab2_words, t
         def load_tab(a):
             nc.sync.dma_start(out=tab_w[a][:], in_=tab_words[a].rearrange("p t i -> p (t i)").bitcast(I32))
 
+        def load_place(n):
+            b, t = divmod(n, 4)
+            rows = place[BANK * b : BANK * (b + 1), :].rearrange("(p t) j -> p t j", t=4)
+            nc.sync.dma_start(out=place_sb[b][:, t, :], in_=rows[:, t, :])
+
         nc.sync.dma_start(idx2[:], offs2)
+        load_w2(0)
+        load_scales(w1_s, w1_scales)
         nc.sync.dma_start(out=tab2_w[:], in_=tab2_words[0].rearrange("p t i -> p (t i)").bitcast(I32))
         for q in range(4):
             nc.sync.dma_start(out=tab2_s[32 * q : 32 * q + 4, :].bitcast(I32), in_=tab2_scales[0, 4 * q : 4 * q + 4, :].bitcast(I32))
-        load_w2(0)
-        nc.sync.dma_start(p1[:], pos1)
-        load_cap(0, 0)
+        load_cap(0)
         load_wgs(0)
+        nc.sync.dma_start(p1[:], pos1)
         nc.sync.dma_start(idx[:], offs)
         for q in range(4):
             nc.sync.dma_start(out=tab_s[32 * q : 32 * q + 8, :].bitcast(I32), in_=tab_scales[:, 4 * q : 4 * q + 4, :].bitcast(I32))
-        load_w2(1)
         load_tab(0)
-        load_scales(w1_s, w1_scales)
         nc.sync.dma_start(out=w1_w[:].bitcast(I32), in_=w1_words.bitcast(I32).rearrange("a p c -> p a c"))
         load_tab(1)
-        nc.sync.dma_start(out=gain_sb[:], in_=gain.rearrange("(b p t) -> p b t", b=2, t=4))
-        load_cap(0, 1)
+        load_cap(2)
         load_wgs(1)
-        load_cap(1, 0)
-        load_cap(1, 1)
+        nc.sync.dma_start(out=gain_sb[:], in_=gain.rearrange("(b p t) -> p b t", b=2, t=4))
+        load_w2(1)
+        for n in range(5):
+            load_place(n)
+            if n + 4 < 8:
+                load_cap(n + 4)
         load_scales(w3_s, w3_scales)
         nc.sync.dma_start(out=w3_w[:], in_=w3_words.rearrange("a p c i -> p a (c i)").bitcast(I32))
-        for h in range(2):
-            for b in range(2):
-                rows = place[BANK * b : BANK * (b + 1), :].rearrange("(p t) j -> p t j", t=4)
-                nc.sync.dma_start(out=place_sb[h, b][:], in_=rows[:, :, HALF * h : HALF * (h + 1)])
+        for n in range(5, 8):
+            load_place(n)
 
-        nc.vector.tensor_copy(v2_w[:], tab2_w[:].bitcast(U32).indirect(idx2[:]))
-        nc.vector.tensor_copy(v2_s[:], tab2_s[:].indirect(idx2[:]))
 
         w2_q = {}
 
@@ -133,129 +134,154 @@ def tile_list_hull_drag_features_kernel(tc, tab_words, tab_scales, tab2_words, t
             w2_q[b, u] = (codes, scales)
 
         limited = {}
+        weighed = {}
 
-        def limit(b, t):
+        def limit(n):
+            b, t = divmod(n, 4)
             codes, scales = w2_q[b, t // 2]
             cols = slice(P * (t % 2), P * (t % 2 + 1))
             acc = psum.tile([P, BANK], F32, name="acc_b", tag="acc_by", bufs=4)
             nc.tensor.matmul_mx(out=acc[:], lhsT=codes[:, cols].bitcast(FP8X4), lhsT_scale=scales[:, cols],
                                 rhs=v2_w[:].bitcast(FP8X4), rhs_scale=v2_s[:], start=True, stop=True)
-            low = ring.tile([P, P2], F32, name="low", bufs=3)
-            nc.vector.tensor_tensor(out=low[:], in0=acc[:], in1=cap_sb[b, t // 2][:, t % 2, :], op=ALU.min)
-            limited[b, t] = low
+            first = max(start for start in cap_sb if start <= n)
+            limited[n] = ring.tile([P, P2], F32, name="low")
+            nc.vector.tensor_tensor(out=limited[n][:], in0=acc[:], in1=cap_sb[first][:, n - first, :], op=ALU.min)
 
-        def put(b, t):
-            nc.vector.tensor_tensor(pages[b, t][:].indirect(p1[:]), limited[b, t][:], wgs_sb[t // 2][:, t % 2, :], ALU.mult)
+        def wgs_rows(n):
+            return wgs_sb[n % 4 // 2][:, n % 2, :]
+
+        def weigh(n):
+            weighed[n] = ring.tile([P, P2], F32, name="weighed", bufs=3)
+            nc.gpsimd.tensor_tensor(out=weighed[n][:], in0=limited[n][:], in1=wgs_rows(n), op=ALU.mult)
+
+        def put(n):
+            nc.vector.tensor_copy(pages[n % 3][:].indirect(p1[:]), weighed[n][:])
+
+        def scale_by_place(n):
+            rows = place_sb[n // 4][:, n % 4, :]
+            nc.gpsimd.tensor_tensor(out=rows, in0=pages[n % 3][:], in1=rows, op=ALU.mult)
 
         quantise_w2(0, 0, True)
         quantise_w2(0, 1, False)
-        limit(0, 0)
-        limit(0, 1)
-        put(0, 0)
-        put(0, 1)
-
+        nc.vector.tensor_copy(v2_w[:], tab2_w[:].bitcast(U32).indirect(idx2[:]))
+        nc.vector.tensor_copy(v2_s[:], tab2_s[:].indirect(idx2[:]))
+        limit(0)
+        limit(1)
+        nc.vector.tensor_tensor(pages[0][:].indirect(p1[:]), limited[0][:], wgs_rows(0), ALU.mult)
+        weigh(1)
         nc.vector.tensor_copy(v_s[0][:], tab_s[:].indirect(idx[:]))
         for q in range(4):
             nc.scalar.dma_start(out=v_s[1][32 * q : 32 * q + 4, :].bitcast(I32), in_=v_s[0][32 * q + 4 : 32 * q + 8, :].bitcast(I32))
-        quantise_w2(1, 0, False)
-        quantise_w2(1, 1, False)
-        for t in range(4):
-            pages[1, t] = shared.tile([P, S], F32, name=f"page1{t}", offset=8 * T + 4 * S * t)
-            nc.gpsimd.memset(pages[1, t][:], 0.0)
+
+        w1_dealt = []
+        for b in range(2):
+            words = keep.tile([P, 2, 2 * BANK], U8, name=f"w1_dealt_w{b}", align_bytes=64)
+            scales = shared.tile([P, 2, BANK], U8, name=f"w1_dealt_s{b}", align_bytes=64, offset=10 * T + 2 * BANK * b)
+            nc.gpsimd.tensor_copy(out=scales[:].rearrange("p a (t q) -> p a t q", t=4),
+                                  in_=w1_s[:, :, BANK * b : BANK * (b + 1)].rearrange("p a (q t) -> p a t q", t=4))
+            nc.scalar.copy(out=words[:].bitcast(U16).rearrange("p a (t q) -> p a t q", t=4),
+                           in_=w1_w[:].bitcast(U16)[:, :, BANK * b : BANK * (b + 1)].rearrange("p a (q t) -> p a t q", t=4))
+            w1_dealt.append((words, scales))
+
         nc.vector.tensor_copy(v_w[0][:], tab_w[0][:].bitcast(U32).indirect(idx[:]))
         for h in range(2):
             nc.vector.tensor_copy(v_w[1][:, HALF * h : HALF * (h + 1)],
                                   tab_w[1][:].bitcast(U32).indirect(idx[:, HALF // 16 * h : HALF // 16 * (h + 1)]))
-
-        slices = [(0, 2), (0, 3), (1, 0), (1, 1), (1, 2), (1, 3)]
-        limit(*slices[0])
-        for now, ahead in zip(slices, slices[1:] + [None]):
-            if ahead is not None:
-                limit(*ahead)
-            put(*now)
+        for n in (1, 2):
+            pages.append(shared.tile([P, S], F32, name=f"page{n}", offset=4 * T + 4 * S * (n + 1)))
+            nc.gpsimd.memset(pages[n][:], 0.0)
+        for n in (2, 3):
+            limit(n)
+            weigh(n)
+        put(1)
+        put(2)
+        quantise_w2(1, 0, False)
+        quantise_w2(1, 1, False)
+        for n in range(3, 8):
+            scale_by_place(n - 3)
+            if n + 1 < 8:
+                limit(n + 1)
+                weigh(n + 1)
+            put(n)
+        scale_by_place(5)
+        scale_by_place(6)
 
         a_sb = {}
-        roots = {}
 
-        def square(h, b, jt):
-            if jt == 0:
-                roots[h, b] = ring.tile([P, 4, BANK], F32, name="root")
-            cols = slice(HALF * h + P * jt, HALF * h + P * (jt + 1))
-            acc = psum.tile([P, BANK], F32, name="acc_rough")
+        def square(h, b, t):
+            if t == 0:
+                a_sb[h, b] = shared.tile([P, 4, HALF], F32, name=f"a{h}{b}", offset=A_OFFSETS[2 * h + b])
+            words, scales = w1_dealt[b]
+            cols = slice(HALF * h, HALF * (h + 1))
+            acc = psum.tile([P, BANK], F32, name="acc_rough", bufs=4)
             for a in range(2):
-                nc.tensor.matmul_mx(out=acc[:], lhsT=v_w[a][:, cols].bitcast(FP8X4), lhsT_scale=v_s[a][:, cols],
-                                    rhs=w1_w[:, a, 2 * BANK * b : 2 * BANK * (b + 1)].bitcast(FP4X4),
-                                    rhs_scale=w1_s[:, a, BANK * b : BANK * (b + 1)], start=(a == 0), stop=(a == 1))
-            nc.scalar.activation(out=roots[h, b][:, jt, :].rearrange("p (t q) -> p t q", t=4),
-                                 in_=acc[:].rearrange("p (q t) -> p t q", t=4), func=ACT.Square)
+                nc.tensor.matmul_mx(out=acc[:], lhsT=words[:, a, 2 * P * t : 2 * P * (t + 1)].bitcast(FP4X4),
+                                    lhsT_scale=scales[:, a, P * t : P * (t + 1)],
+                                    rhs=v_w[a][:, cols].bitcast(FP8X4), rhs_scale=v_s[a][:, cols], start=(a == 0), stop=(a == 1))
+            nc.scalar.activation(out=a_sb[h, b][:, t, :], in_=acc[:], func=ACT.Square)
 
         def root(h, b):
-            whole = roots[h, b][:].rearrange("p jt c -> p (jt c)")
+            whole = a_sb[h, b][:].rearrange("p t c -> p (t c)")
             nc.scalar.activation(out=whole, in_=whole, func=ACT.Sqrt, bias=1.0)
 
-        def turn(h, b, t):
-            if t == 0:
-                a_sb[h, b] = shared.tile([P, 4, HALF], F32, name=f"a{h}{b}", offset=4 * 4 * HALF * (2 * h + b))
-            turned = psum.tile([P, BANK], F32, name="turned")
-            for jt in range(4):
-                nc.tensor.transpose(turned[:, P * jt : P * (jt + 1)], roots[h, b][:, jt, P * t : P * (t + 1)], ident[:])
-            nc.scalar.activation(out=a_sb[h, b][:, t, :], in_=turned[:], func=ACT.Copy, scale=gain_sb[:, b, t : t + 1])
+        def apply_gain(h, b, t):
+            rows = a_sb[h, b][:, t, :]
+            nc.scalar.activation(out=rows, in_=rows, func=ACT.Copy, scale=gain_sb[:, b, t : t + 1])
 
         units = [(h, b) for h in range(2) for b in range(2)]
         for before, now in zip([None] + units, units + [None]):
-            for pair in range(2):
-                for x in (2 * pair, 2 * pair + 1):
-                    if now is not None:
-                        square(*now, x)
-                for x in (2 * pair, 2 * pair + 1):
-                    if before is not None:
-                        turn(*before, x)
+            for t in range(4):
+                if now is not None:
+                    square(*now, t)
+                if before is not None:
+                    apply_gain(*before, t)
             if now is not None:
                 root(*now)
 
         z_bf = {}
-        scaled = {}
-        all_rows = [(b, t) for b in range(2) for t in range(4)]
+        z_q = {}
 
-        def scale_by_place(c0, w, rows):
+        def add_up(c0, w, b):
             h, local = c0 // HALF, slice(c0 % HALF, c0 % HALF + w)
-            if c0 not in scaled:
-                scaled[c0] = ring.tile([P, 2, 4, w], F32, name="scaled")
-            for b, t in rows:
-                nc.vector.tensor_tensor(out=scaled[c0][:, b, t, :], in0=pages[b, t][:, c0 : c0 + w], in1=place_sb[h, b][:, t, local], op=ALU.mult)
+            z_bf[c0, b] = ring.tile([P, w, 4], BF16, name="z_bf", align_bytes=64, bufs=3)
+            nc.vector.tensor_tensor(out=z_bf[c0, b][:].rearrange("p (c i) t -> p c t i", i=RUN),
+                                    in0=a_sb[h, b][:, :, local].rearrange("p t (c i) -> p c t i", i=RUN),
+                                    in1=place_sb[b][:, :, c0 : c0 + w].rearrange("p t (c i) -> p c t i", i=RUN), op=ALU.add)
 
-        def add_up(c0, w):
-            h, local = c0 // HALF, slice(c0 % HALF, c0 % HALF + w)
-            z = ring.tile([P, 2, w, 4], BF16, name="z_bf", align_bytes=64)
-            for b in range(2):
-                nc.vector.tensor_tensor(out=z[:, b].rearrange("p (c i) t -> p c t i", i=RUN),
-                                        in0=a_sb[h, b][:, :, local].rearrange("p t (c i) -> p c t i", i=RUN),
-                                        in1=scaled[c0][:, b].rearrange("p t (c i) -> p c t i", i=RUN), op=ALU.add)
-            z_bf[c0] = z
+        def quantise_z(c0, w, b):
+            codes = ring.tile([P, w], U32, name="z_codes", align_bytes=64, bufs=4)
+            scales = ring.tile([P, w], U8, name="z_scales", align_bytes=64, bufs=4)
+            nc.vector.quantize_mx(out=codes[:].bitcast(FP8X4), scales=scales[:], in_=z_bf[c0, b][:].rearrange("p c t -> p (c t)"))
+            z_q[c0, b] = (codes, scales)
 
-        def finish(c0, w):
-            codes = ring.tile([P, 2 * w], U32, name="z_codes", align_bytes=64)
-            scales = ring.tile([P, 2 * w], U8, name="z_scales", align_bytes=64)
-            nc.vector.quantize_mx(out=codes[:].bitcast(FP8X4), scales=scales[:], in_=z_bf[c0][:].rearrange("p b c t -> p (b c t)"))
-            res = ring.tile([P, 4 * w], F32, name="res", tag="cap_out", bufs=4)
-            per_bank = BANK // w
-            for first in range(0, 4, per_bank):
-                acc = psum.tile([P, BANK], F32, name="acc_y", tag="acc_by", bufs=4)
-                for g in range(per_bank):
-                    cols = slice(P * (first + g), P * (first + g + 1))
+        def finish(c0, w, groups):
+            res = ring.tile([P, len(groups), w], F32, name="res", tag="cap_out", bufs=6)
+            for first in range(0, len(groups), 2 if w == 256 else 4):
+                bank = groups[first : first + BANK // w]
+                acc = psum.tile([P, len(bank), w], F32, name="acc_y", tag="acc_by", bufs=4)
+                for place_in_bank, g in enumerate(bank):
+                    cols = slice(P * g, P * (g + 1))
                     for b in range(2):
-                        nc.tensor.matmul_mx(out=acc[:, w * g : w * (g + 1)], lhsT=w3_w[:, b, cols].bitcast(FP8X4), lhsT_scale=w3_s[:, b, cols],
-                                            rhs=codes[:, w * b : w * (b + 1)].bitcast(FP8X4), rhs_scale=scales[:, w * b : w * (b + 1)],
-                                            start=(b == 0), stop=(b == 1))
-                nc.scalar.activation(out=res[:, w * first : w * first + BANK], in_=acc[:], func=ACT.Abs)
+                        codes, scales = z_q[c0, b]
+                        nc.tensor.matmul_mx(out=acc[:, place_in_bank, :], lhsT=w3_w[:, b, cols].bitcast(FP8X4), lhsT_scale=w3_s[:, b, cols],
+                                            rhs=codes[:].bitcast(FP8X4), rhs_scale=scales[:], start=(b == 0), stop=(b == 1))
+                nc.scalar.activation(out=res[:, first : first + len(bank), :], in_=acc[:], func=ACT.Abs)
             nc.scalar.activation(out=res[:], in_=res[:], func=ACT.Ln, bias=1.0)
-            nc.sync.dma_start(out=out.rearrange("(g p) j -> p g j", p=P)[:, :, c0 : c0 + w], in_=res[:].rearrange("p (g j) -> p g j", g=4))
+            nc.sync.dma_start(out=out.rearrange("(g p) j -> p g j", p=P)[:, groups[0] : groups[-1] + 1, c0 : c0 + w], in_=res[:])
 
         for before, now in zip([None] + CHUNKS, CHUNKS + [None]):
             if now is not None:
-                scale_by_place(*now, all_rows[:1])
+                c0, w = now
+                last_rows = place_sb[1][:, 3, c0 : c0 + w]
+                nc.vector.tensor_tensor(out=last_rows, in0=pages[7 % 3][:, c0 : c0 + w], in1=last_rows, op=ALU.mult)
+                add_up(*now, 0)
             if before is not None:
-                finish(*before)
+                quantise_z(*before, 1)
+                if now is not None:
+                    finish(*before, [0, 1, 2, 3])
+                else:
+                    finish(*before, [0, 1])
+                    finish(*before, [2, 3])
             if now is not None:
-                scale_by_place(*now, all_rows[1:])
-                add_up(*now)
+                add_up(*now, 1)
+                quantise_z(*now, 0)

@@ -19,9 +19,11 @@ ALU = mybir.AluOpType
 P = 128
 BANK = 512
 HALF = S // 2
-CHUNKS = [(0, 256), (256, 256), (512, 256), (768, 128), (896, 128)]
+CHUNK = 128
+CHUNKS = [((HALF + c0) % S, CHUNK) for c0 in range(0, S, CHUNK)]
 RUN = 4
 CAP_LOADS = [(0, 2), (2, 2), (4, 1), (5, 1), (6, 1), (7, 1)]
+WGS_LOADS = [(0, 2), (2, 2)]
 A_OFFSETS = [0, 2 * T, 4 * T, 8 * T]
 
 
@@ -51,22 +53,23 @@ def tile_list_hull_drag_features_kernel(tc, tab_words, tab_scales, tab2_words, t
         w1_s = keep.tile([P, 2, H], U8, name="w1_s", align_bytes=64)
         w3_w = keep.tile([P, 2, N], I32, name="w3_w", align_bytes=64)
         w3_s = keep.tile([P, 2, N], U8, name="w3_s", align_bytes=64)
-        w2_raw = [shared.tile([P, 4, BANK], F32, name="w2_raw0", offset=10 * T), keep.tile([P, 4, BANK], F32, name="w2_raw1")]
+        w2_raw = [keep.tile([P, 4, BANK], F32, name=f"w2_raw{b}") for b in range(2)]
         gain_sb = keep.tile([P, 2, 4], F32, name="gain_sb")
-        wgs_sb = [keep.tile([P, 2, P2], F32, name=f"wgs{u}") for u in range(2)]
+        wgs_sb = {first: keep.tile([P, count, P2], F32, name=f"wgs{first}") for first, count in WGS_LOADS}
         cap_sb = {first: ring.tile([P, count, P2], F32, name=f"cap{first}", tag="cap_out", bufs=6) for first, count in CAP_LOADS}
         place_sb = [keep.tile([P, 4, S], F32, name=f"place{b}") for b in range(2)]
-        pages = [keep.tile([P, S], F32, name="page0")]
+        pages = [keep.tile([P, S], F32, name=f"page{n}") for n in range(4)]
 
         nc.gpsimd.memset(tab2_s[:].bitcast(I32), 0)
         for tile_s in (w1_s, tab_s, w3_s, v_s[1]):
             nc.vector.memset(tile_s[:].bitcast(I32), 0)
-        nc.vector.memset(pages[0][:], 0.0)
+        for page in pages:
+            nc.vector.memset(page[:], 0.0)
 
-        def load_scales(tile_s, dram):
+        def load_scales(queue, tile_s, dram):
             rows = dram.bitcast(I32).rearrange("a (q r) c -> q r a c", r=4)
             for q in range(4):
-                nc.sync.dma_start(out=tile_s[32 * q : 32 * q + 4].bitcast(I32), in_=rows[q])
+                queue.dma_start(out=tile_s[32 * q : 32 * q + 4].bitcast(I32), in_=rows[q])
 
         def load_w2(b):
             nc.sync.dma_start(out=w2_raw[b][:], in_=w2.rearrange("(p j) c -> p j c", j=4)[:, :, BANK * b : BANK * (b + 1)])
@@ -76,10 +79,10 @@ def tile_list_hull_drag_features_kernel(tc, tab_words, tab_scales, tab2_words, t
             rows = cap[BANK * b : BANK * (b + 1), :].rearrange("(p t) j -> p t j", t=4)
             nc.sync.dma_start(out=cap_sb[first][:], in_=rows[:, t : t + dict(CAP_LOADS)[first], :])
 
-        def load_wgs(u):
-            rows = wgs.rearrange("(p t) j -> p t j", t=4)[:, 2 * u : 2 * u + 2, :]
+        def load_wgs(first):
+            rows = wgs.rearrange("(p t) j -> p t j", t=4)[:, first : first + dict(WGS_LOADS)[first], :]
             for q in range(4):
-                nc.sync.dma_start(out=wgs_sb[u][32 * q : 32 * (q + 1)], in_=rows)
+                nc.sync.dma_start(out=wgs_sb[first][32 * q : 32 * (q + 1)], in_=rows)
 
         def load_tab(a):
             nc.sync.dma_start(out=tab_w[a][:], in_=tab_words[a].rearrange("p t i -> p (t i)").bitcast(I32))
@@ -89,15 +92,20 @@ def tile_list_hull_drag_features_kernel(tc, tab_words, tab_scales, tab2_words, t
             rows = place[BANK * b : BANK * (b + 1), :].rearrange("(p t) j -> p t j", t=4)
             nc.sync.dma_start(out=place_sb[b][:, t, :], in_=rows[:, t, :])
 
+        def load_place_half(h):
+            rows = place[BANK:, :].rearrange("(p t) j -> p t j", t=4)
+            nc.sync.dma_start(out=place_sb[1][:, :, HALF * h : HALF * (h + 1)], in_=rows[:, :, HALF * h : HALF * (h + 1)])
+
         nc.sync.dma_start(idx2[:], offs2)
-        load_w2(0)
-        load_scales(w1_s, w1_scales)
         nc.sync.dma_start(out=tab2_w[:], in_=tab2_words[0].rearrange("p t i -> p (t i)").bitcast(I32))
         for q in range(4):
             nc.sync.dma_start(out=tab2_s[32 * q : 32 * q + 4, :].bitcast(I32), in_=tab2_scales[0, 4 * q : 4 * q + 4, :].bitcast(I32))
+        load_w2(0)
+        load_scales(nc.sync, w1_s, w1_scales)
         load_cap(0)
         load_wgs(0)
         nc.sync.dma_start(p1[:], pos1)
+        load_w2(1)
         nc.sync.dma_start(idx[:], offs)
         for q in range(4):
             nc.sync.dma_start(out=tab_s[32 * q : 32 * q + 8, :].bitcast(I32), in_=tab_scales[:, 4 * q : 4 * q + 4, :].bitcast(I32))
@@ -105,36 +113,30 @@ def tile_list_hull_drag_features_kernel(tc, tab_words, tab_scales, tab2_words, t
         nc.sync.dma_start(out=w1_w[:].bitcast(I32), in_=w1_words.bitcast(I32).rearrange("a p c -> p a c"))
         load_tab(1)
         load_cap(2)
-        load_wgs(1)
+        load_wgs(2)
         nc.sync.dma_start(out=gain_sb[:], in_=gain.rearrange("(b p t) -> p b t", b=2, t=4))
-        load_w2(1)
-        for n in range(5):
+        for n in range(4):
             load_place(n)
-            if n + 4 < 8:
-                load_cap(n + 4)
-        load_scales(w3_s, w3_scales)
+            load_cap(n + 4)
+        load_scales(nc.sync, w3_s, w3_scales)
         nc.sync.dma_start(out=w3_w[:], in_=w3_words.rearrange("a p c i -> p a (c i)").bitcast(I32))
-        for n in range(5, 8):
-            load_place(n)
+        load_place_half(1)
+        load_place_half(0)
 
 
         w2_q = {}
 
-        def quantise_w2(b, u, on_vector):
+        def quantise_w2(b, u, copy):
             grouped = ring.tile([P, 2, P, 4], BF16, name="w2_grouped", align_bytes=64, bufs=4)
             src = w2_raw[b][:].rearrange("p j (m t) -> p m j t", t=4)[:, :, :, 2 * u : 2 * u + 2]
             dst = grouped[:].rearrange("p t m j -> p m j t")
-            if on_vector:
-                nc.vector.tensor_copy(out=dst, in_=src)
-            else:
-                nc.scalar.copy(out=dst, in_=src)
+            copy(out=dst, in_=src)
             codes = keep.tile([P, 2 * P], U32, name=f"w2_codes{b}{u}", align_bytes=64)
             scales = keep.tile([P, 2 * P], U8, name=f"w2_scales{b}{u}", align_bytes=64)
             nc.vector.quantize_mx(out=codes[:].bitcast(FP8X4), scales=scales[:], in_=grouped[:].rearrange("p t m j -> p (t m j)"))
             w2_q[b, u] = (codes, scales)
 
         limited = {}
-        weighed = {}
 
         def limit(n):
             b, t = divmod(n, 4)
@@ -144,67 +146,52 @@ def tile_list_hull_drag_features_kernel(tc, tab_words, tab_scales, tab2_words, t
             nc.tensor.matmul_mx(out=acc[:], lhsT=codes[:, cols].bitcast(FP8X4), lhsT_scale=scales[:, cols],
                                 rhs=v2_w[:].bitcast(FP8X4), rhs_scale=v2_s[:], start=True, stop=True)
             first = max(start for start in cap_sb if start <= n)
-            limited[n] = ring.tile([P, P2], F32, name="low")
+            limited[n] = ring.tile([P, P2], F32, name="low", tag="low_z", align_bytes=64, bufs=3)
             nc.vector.tensor_tensor(out=limited[n][:], in0=acc[:], in1=cap_sb[first][:, n - first, :], op=ALU.min)
 
-        def wgs_rows(n):
-            return wgs_sb[n % 4 // 2][:, n % 2, :]
-
-        def weigh(n):
-            weighed[n] = ring.tile([P, P2], F32, name="weighed", bufs=3)
-            nc.gpsimd.tensor_tensor(out=weighed[n][:], in0=limited[n][:], in1=wgs_rows(n), op=ALU.mult)
-
         def put(n):
-            nc.vector.tensor_copy(pages[n % 3][:].indirect(p1[:]), weighed[n][:])
+            first = n % 4 // 2 * 2
+            nc.vector.tensor_tensor(pages[n % 4][:].indirect(p1[:]), limited[n][:], wgs_sb[first][:, n % 4 - first, :], ALU.mult)
 
-        def scale_by_place(n):
-            rows = place_sb[n // 4][:, n % 4, :]
-            nc.gpsimd.tensor_tensor(out=rows, in0=pages[n % 3][:], in1=rows, op=ALU.mult)
+        def scale_by_place(t):
+            nc.vector.tensor_tensor(out=place_sb[0][:, t, :], in0=pages[t][:], in1=place_sb[0][:, t, :], op=ALU.mult)
 
-        quantise_w2(0, 0, True)
-        quantise_w2(0, 1, False)
         nc.vector.tensor_copy(v2_w[:], tab2_w[:].bitcast(U32).indirect(idx2[:]))
         nc.vector.tensor_copy(v2_s[:], tab2_s[:].indirect(idx2[:]))
-        limit(0)
-        limit(1)
-        nc.vector.tensor_tensor(pages[0][:].indirect(p1[:]), limited[0][:], wgs_rows(0), ALU.mult)
-        weigh(1)
-        nc.vector.tensor_copy(v_s[0][:], tab_s[:].indirect(idx[:]))
-        for q in range(4):
-            nc.scalar.dma_start(out=v_s[1][32 * q : 32 * q + 4, :].bitcast(I32), in_=v_s[0][32 * q + 4 : 32 * q + 8, :].bitcast(I32))
-
+        quantise_w2(0, 0, nc.vector.tensor_copy)
+        quantise_w2(0, 1, nc.scalar.copy)
         w1_dealt = []
         for b in range(2):
             words = keep.tile([P, 2, 2 * BANK], U8, name=f"w1_dealt_w{b}", align_bytes=64)
-            scales = shared.tile([P, 2, BANK], U8, name=f"w1_dealt_s{b}", align_bytes=64, offset=10 * T + 2 * BANK * b)
-            nc.gpsimd.tensor_copy(out=scales[:].rearrange("p a (t q) -> p a t q", t=4),
+            scales = keep.tile([P, 2, BANK], U8, name=f"w1_dealt_s{b}", align_bytes=64)
+            nc.vector.tensor_copy(out=scales[:].rearrange("p a (t q) -> p a t q", t=4),
                                   in_=w1_s[:, :, BANK * b : BANK * (b + 1)].rearrange("p a (q t) -> p a t q", t=4))
             nc.scalar.copy(out=words[:].bitcast(U16).rearrange("p a (t q) -> p a t q", t=4),
                            in_=w1_w[:].bitcast(U16)[:, :, BANK * b : BANK * (b + 1)].rearrange("p a (q t) -> p a t q", t=4))
             w1_dealt.append((words, scales))
 
+        limit(0)
+        limit(1)
+        put(0)
+        put(1)
+        quantise_w2(1, 0, nc.scalar.copy)
+        quantise_w2(1, 1, nc.scalar.copy)
+        nc.vector.tensor_copy(v_s[0][:], tab_s[:].indirect(idx[:]))
+        for q in range(4):
+            nc.scalar.dma_start(out=v_s[1][32 * q : 32 * q + 4, :].bitcast(I32), in_=v_s[0][32 * q + 4 : 32 * q + 8, :].bitcast(I32))
         nc.vector.tensor_copy(v_w[0][:], tab_w[0][:].bitcast(U32).indirect(idx[:]))
         for h in range(2):
             nc.vector.tensor_copy(v_w[1][:, HALF * h : HALF * (h + 1)],
                                   tab_w[1][:].bitcast(U32).indirect(idx[:, HALF // 16 * h : HALF // 16 * (h + 1)]))
-        for n in (1, 2):
-            pages.append(shared.tile([P, S], F32, name=f"page{n}", offset=4 * T + 4 * S * (n + 1)))
-            nc.gpsimd.memset(pages[n][:], 0.0)
-        for n in (2, 3):
-            limit(n)
-            weigh(n)
-        put(1)
+        limit(2)
+        limit(3)
         put(2)
-        quantise_w2(1, 0, False)
-        quantise_w2(1, 1, False)
         for n in range(3, 8):
-            scale_by_place(n - 3)
+            if n >= 4:
+                scale_by_place(n - 4)
             if n + 1 < 8:
                 limit(n + 1)
-                weigh(n + 1)
             put(n)
-        scale_by_place(5)
-        scale_by_place(6)
 
         a_sb = {}
 
@@ -241,20 +228,29 @@ def tile_list_hull_drag_features_kernel(tc, tab_words, tab_scales, tab2_words, t
         z_bf = {}
         z_q = {}
 
-        def add_up(c0, w, b):
-            h, local = c0 // HALF, slice(c0 % HALF, c0 % HALF + w)
-            z_bf[c0, b] = ring.tile([P, w, 4], BF16, name="z_bf", align_bytes=64, bufs=3)
-            nc.vector.tensor_tensor(out=z_bf[c0, b][:].rearrange("p (c i) t -> p c t i", i=RUN),
-                                    in0=a_sb[h, b][:, :, local].rearrange("p t (c i) -> p c t i", i=RUN),
-                                    in1=place_sb[b][:, :, c0 : c0 + w].rearrange("p t (c i) -> p c t i", i=RUN), op=ALU.add)
+        scaled = {}
 
-        def quantise_z(c0, w, b):
-            codes = ring.tile([P, w], U32, name="z_codes", align_bytes=64, bufs=4)
-            scales = ring.tile([P, w], U8, name="z_scales", align_bytes=64, bufs=4)
-            nc.vector.quantize_mx(out=codes[:].bitcast(FP8X4), scales=scales[:], in_=z_bf[c0, b][:].rearrange("p c t -> p (c t)"))
-            z_q[c0, b] = (codes, scales)
+        def scale_chunk(c0, w, t):
+            if t == 0:
+                scaled[c0] = ring.tile([P, 4, w], F32, name="scaled")
+            nc.vector.tensor_tensor(out=scaled[c0][:, t, :], in0=pages[t][:, c0 : c0 + w], in1=place_sb[1][:, t, c0 : c0 + w], op=ALU.mult)
+
+        def add_up(c0, w):
+            h, local = c0 // HALF, slice(c0 % HALF, c0 % HALF + w)
+            z_bf[c0] = ring.tile([P, 2, w, 4], BF16, name="z_bf", tag="low_z", align_bytes=64, bufs=3)
+            for b, placed in enumerate((place_sb[0][:, :, c0 : c0 + w], scaled[c0][:])):
+                nc.vector.tensor_tensor(out=z_bf[c0][:, b].rearrange("p (c i) t -> p c t i", i=RUN),
+                                        in0=a_sb[h, b][:, :, local].rearrange("p t (c i) -> p c t i", i=RUN),
+                                        in1=placed.rearrange("p t (c i) -> p c t i", i=RUN), op=ALU.add)
+
+        def quantise_z(c0, w):
+            codes = ring.tile([P, 2 * w], U32, name="z_codes", align_bytes=64, bufs=3)
+            scales = ring.tile([P, 2 * w], U8, name="z_scales", align_bytes=64, bufs=3)
+            nc.vector.quantize_mx(out=codes[:].bitcast(FP8X4), scales=scales[:], in_=z_bf[c0][:].rearrange("p b c t -> p (b c t)"))
+            z_q[c0] = (codes, scales)
 
         def finish(c0, w, groups):
+            codes, scales = z_q[c0]
             res = ring.tile([P, len(groups), w], F32, name="res", tag="cap_out", bufs=6)
             for first in range(0, len(groups), 2 if w == 256 else 4):
                 bank = groups[first : first + BANK // w]
@@ -262,26 +258,21 @@ def tile_list_hull_drag_features_kernel(tc, tab_words, tab_scales, tab2_words, t
                 for place_in_bank, g in enumerate(bank):
                     cols = slice(P * g, P * (g + 1))
                     for b in range(2):
-                        codes, scales = z_q[c0, b]
                         nc.tensor.matmul_mx(out=acc[:, place_in_bank, :], lhsT=w3_w[:, b, cols].bitcast(FP8X4), lhsT_scale=w3_s[:, b, cols],
-                                            rhs=codes[:].bitcast(FP8X4), rhs_scale=scales[:], start=(b == 0), stop=(b == 1))
+                                            rhs=codes[:, w * b : w * (b + 1)].bitcast(FP8X4), rhs_scale=scales[:, w * b : w * (b + 1)],
+                                            start=(b == 0), stop=(b == 1))
                 nc.scalar.activation(out=res[:, first : first + len(bank), :], in_=acc[:], func=ACT.Abs)
             nc.scalar.activation(out=res[:], in_=res[:], func=ACT.Ln, bias=1.0)
             nc.sync.dma_start(out=out.rearrange("(g p) j -> p g j", p=P)[:, groups[0] : groups[-1] + 1, c0 : c0 + w], in_=res[:])
 
         for before, now in zip([None] + CHUNKS, CHUNKS + [None]):
             if now is not None:
-                c0, w = now
-                last_rows = place_sb[1][:, 3, c0 : c0 + w]
-                nc.vector.tensor_tensor(out=last_rows, in0=pages[7 % 3][:, c0 : c0 + w], in1=last_rows, op=ALU.mult)
-                add_up(*now, 0)
+                scale_chunk(*now, 0)
             if before is not None:
-                quantise_z(*before, 1)
-                if now is not None:
-                    finish(*before, [0, 1, 2, 3])
-                else:
-                    finish(*before, [0, 1])
-                    finish(*before, [2, 3])
+                quantise_z(*before)
+                for groups in ([[0, 1, 2, 3]] if now is not None else [[0, 1], [2, 3]]):
+                    finish(*before, groups)
             if now is not None:
-                add_up(*now, 1)
-                quantise_z(*now, 0)
+                for t in range(1, 4):
+                    scale_chunk(*now, t)
+                add_up(*now)

@@ -1,6 +1,7 @@
 from contextlib import ExitStack
 
 import concourse.mybir as mybir
+from concourse.masks import make_identity
 
 K, K2, T, T3, S, P2, H, N = 1024, 512, 4096, 2048, 1024, 512, 1024, 512
 FLOPS = 2 * (K * H * S + K2 * H * P2 + H * N * S)
@@ -17,14 +18,11 @@ ACT = mybir.ActivationFunctionType
 ALU = mybir.AluOpType
 
 P = 128
-BANK = 512
+PASS = 512
 HALF = S // 2
 CHUNK = 128
-CHUNKS = [((HALF + c0) % S, CHUNK) for c0 in range(0, S, CHUNK)]
 RUN = 4
-CAP_LOADS = [(0, 2), (2, 2), (4, 1), (5, 1), (6, 1), (7, 1)]
-WGS_LOADS = [(0, 2), (2, 2)]
-A_OFFSETS = [0, 2 * T, 4 * T, 8 * T]
+V2_SCALE_ROW = 8
 
 
 def tile_list_hull_drag_features_kernel(tc, tab_words, tab_scales, tab2_words, tab2_scales, offs, offs2, pos1,
@@ -35,13 +33,13 @@ def tile_list_hull_drag_features_kernel(tc, tab_words, tab_scales, tab2_words, t
         keep = ctx.enter_context(tc.tile_pool(name="keep", bufs=1))
         shared = ctx.enter_context(tc.tile_pool(name="shared", bufs=1))
         ring = ctx.enter_context(tc.tile_pool(name="ring", bufs=2))
-        psum = ctx.enter_context(tc.psum_pool(name="psum", bufs=2))
+        psum = ctx.enter_context(tc.psum_pool(name="psum", bufs=4))
 
         idx = lists.tile([P, S // 16], U16, name="idx")
         idx2 = lists.tile([P, P2 // 16], U16, name="idx2")
         p1 = lists.tile([P, P2 // 16], U16, name="p1")
 
-        tab2_w = shared.tile([P, T3], I32, name="tab2_w", offset=8 * T)
+        tab2_w = keep.tile([P, T3], I32, name="tab2_w", align_bytes=64)
         tab2_s = keep.tile([P, T3], U8, name="tab2_s", align_bytes=64)
         tab_s = keep.tile([P, T], U8, name="tab_s", align_bytes=64)
         tab_w = [shared.tile([P, T], I32, name=f"tab_w{a}", offset=4 * T * a) for a in range(2)]
@@ -53,170 +51,172 @@ def tile_list_hull_drag_features_kernel(tc, tab_words, tab_scales, tab2_words, t
         w1_s = keep.tile([P, 2, H], U8, name="w1_s", align_bytes=64)
         w3_w = keep.tile([P, 2, N], I32, name="w3_w", align_bytes=64)
         w3_s = keep.tile([P, 2, N], U8, name="w3_s", align_bytes=64)
-        w2_raw = [keep.tile([P, 4, BANK], F32, name=f"w2_raw{b}") for b in range(2)]
+        w2_raw = [keep.tile([P, 4, PASS], F32, name=f"w2_raw{b}") for b in range(2)]
         gain_sb = keep.tile([P, 2, 4], F32, name="gain_sb")
-        wgs_sb = {first: keep.tile([P, count, P2], F32, name=f"wgs{first}") for first, count in WGS_LOADS}
-        cap_sb = {first: ring.tile([P, count, P2], F32, name=f"cap{first}", tag="cap_out", bufs=6) for first, count in CAP_LOADS}
+        wgs_raw = keep.tile([P, P2], F32, name="wgs_raw")
+        wgs_turned = keep.tile([P, 4, 4, P], F32, name="wgs_turned")
+        wgs_sb = [keep.tile([P, P2], F32, name=f"wgs{t}") for t in range(4)]
+        ident = keep.tile([P, P], F32, name="ident")
+        cap_sb = [ring.tile([P, P2], F32, name=f"cap{n}", tag="cap_out", bufs=8) for n in range(8)]
         place_sb = [keep.tile([P, 4, S], F32, name=f"place{b}") for b in range(2)]
-        pages = [keep.tile([P, S], F32, name=f"page{n}") for n in range(4)]
+        pages = [keep.tile([P, S], F32, name=f"page{t}") for t in range(4)]
 
         nc.gpsimd.memset(tab2_s[:].bitcast(I32), 0)
-        for tile_s in (w1_s, tab_s, w3_s, v_s[1]):
-            nc.vector.memset(tile_s[:].bitcast(I32), 0)
+        make_identity(nc, ident[:])
+        for scale_tile in (w1_s, tab_s, w3_s, v_s[1]):
+            nc.vector.memset(scale_tile[:].bitcast(I32), 0)
         for page in pages:
             nc.vector.memset(page[:], 0.0)
 
-        def load_scales(queue, tile_s, dram):
+        def load_weight_scales(scale_tile, dram):
             rows = dram.bitcast(I32).rearrange("a (q r) c -> q r a c", r=4)
             for q in range(4):
-                queue.dma_start(out=tile_s[32 * q : 32 * q + 4].bitcast(I32), in_=rows[q])
+                nc.sync.dma_start(out=scale_tile[32 * q : 32 * q + 4].bitcast(I32), in_=rows[q])
 
         def load_w2(b):
-            nc.sync.dma_start(out=w2_raw[b][:], in_=w2.rearrange("(p j) c -> p j c", j=4)[:, :, BANK * b : BANK * (b + 1)])
+            nc.sync.dma_start(out=w2_raw[b][:], in_=w2.rearrange("(p j) c -> p j c", j=4)[:, :, PASS * b : PASS * (b + 1)])
 
-        def load_cap(first):
-            b, t = divmod(first, 4)
-            rows = cap[BANK * b : BANK * (b + 1), :].rearrange("(p t) j -> p t j", t=4)
-            nc.sync.dma_start(out=cap_sb[first][:], in_=rows[:, t : t + dict(CAP_LOADS)[first], :])
+        def slice_rows(dram, b):
+            return dram[PASS * b : PASS * (b + 1), :].rearrange("(p t) j -> p t j", t=4)
 
-        def load_wgs(first):
-            rows = wgs.rearrange("(p t) j -> p t j", t=4)[:, first : first + dict(WGS_LOADS)[first], :]
-            for q in range(4):
-                nc.sync.dma_start(out=wgs_sb[first][32 * q : 32 * (q + 1)], in_=rows)
+        def load_cap(n):
+            nc.sync.dma_start(out=cap_sb[n][:], in_=slice_rows(cap, n // 4)[:, n % 4, :])
 
         def load_tab(a):
             nc.sync.dma_start(out=tab_w[a][:], in_=tab_words[a].rearrange("p t i -> p (t i)").bitcast(I32))
 
-        def load_place(n):
-            b, t = divmod(n, 4)
-            rows = place[BANK * b : BANK * (b + 1), :].rearrange("(p t) j -> p t j", t=4)
-            nc.sync.dma_start(out=place_sb[b][:, t, :], in_=rows[:, t, :])
-
-        def load_place_half(h):
-            rows = place[BANK:, :].rearrange("(p t) j -> p t j", t=4)
-            nc.sync.dma_start(out=place_sb[1][:, :, HALF * h : HALF * (h + 1)], in_=rows[:, :, HALF * h : HALF * (h + 1)])
-
         nc.sync.dma_start(idx2[:], offs2)
-        nc.sync.dma_start(out=tab2_w[:], in_=tab2_words[0].rearrange("p t i -> p (t i)").bitcast(I32))
-        for q in range(4):
-            nc.sync.dma_start(out=tab2_s[32 * q : 32 * q + 4, :].bitcast(I32), in_=tab2_scales[0, 4 * q : 4 * q + 4, :].bitcast(I32))
+        nc.sync.dma_start(out=wgs_raw[:], in_=wgs)
         load_w2(0)
-        load_scales(nc.sync, w1_s, w1_scales)
+        for q in range(4):
+            first_row = 32 * q + V2_SCALE_ROW
+            nc.sync.dma_start(out=tab2_s[first_row : first_row + 4, :].bitcast(I32), in_=tab2_scales[0, 4 * q : 4 * q + 4, :].bitcast(I32))
+        nc.sync.dma_start(out=tab2_w[:], in_=tab2_words[0].rearrange("p t i -> p (t i)").bitcast(I32))
+        load_weight_scales(w1_s, w1_scales)
         load_cap(0)
-        load_wgs(0)
         nc.sync.dma_start(p1[:], pos1)
-        load_w2(1)
+        load_cap(1)
         nc.sync.dma_start(idx[:], offs)
         for q in range(4):
             nc.sync.dma_start(out=tab_s[32 * q : 32 * q + 8, :].bitcast(I32), in_=tab_scales[:, 4 * q : 4 * q + 4, :].bitcast(I32))
+        load_cap(2)
         load_tab(0)
         nc.sync.dma_start(out=w1_w[:].bitcast(I32), in_=w1_words.bitcast(I32).rearrange("a p c -> p a c"))
         load_tab(1)
-        load_cap(2)
-        load_wgs(2)
+        load_cap(3)
+        load_w2(1)
         nc.sync.dma_start(out=gain_sb[:], in_=gain.rearrange("(b p t) -> p b t", b=2, t=4))
-        for n in range(4):
-            load_place(n)
-            load_cap(n + 4)
-        load_scales(nc.sync, w3_s, w3_scales)
+        for t in range(4):
+            nc.sync.dma_start(out=place_sb[0][:, t, :], in_=slice_rows(place, 0)[:, t, :])
+            load_cap(4 + t)
+        load_weight_scales(w3_s, w3_scales)
         nc.sync.dma_start(out=w3_w[:], in_=w3_words.rearrange("a p c i -> p a (c i)").bitcast(I32))
-        load_place_half(1)
-        load_place_half(0)
+        for h in range(2):
+            half = slice(HALF * h, HALF * (h + 1))
+            nc.sync.dma_start(out=place_sb[1][:, :, half], in_=slice_rows(place, 1)[:, :, half])
 
+        turned = psum.tile([P, 4, P], F32, name="wgs_first_turn", tag="acc_first")
+        for jt in range(4):
+            nc.tensor.transpose(turned[:, jt, :], wgs_raw[:, P * jt : P * (jt + 1)], ident[:])
+        for q in range(4):
+            nc.scalar.copy(out=wgs_turned[:, :, :, 32 * q : 32 * (q + 1)], in_=turned[:].rearrange("p jt (e t) -> p jt t e", t=4))
+        for t in range(4):
+            back = psum.tile([P, P2], F32, name="wgs_second_turn", tag="acc_later")
+            for jt in range(4):
+                nc.tensor.transpose(back[:, P * jt : P * (jt + 1)], wgs_turned[:, jt, t, :], ident[:])
+            nc.scalar.copy(out=wgs_sb[t][:], in_=back[:])
 
         w2_q = {}
 
         def quantise_w2(b, u, copy):
             grouped = ring.tile([P, 2, P, 4], BF16, name="w2_grouped", align_bytes=64, bufs=4)
-            src = w2_raw[b][:].rearrange("p j (m t) -> p m j t", t=4)[:, :, :, 2 * u : 2 * u + 2]
-            dst = grouped[:].rearrange("p t m j -> p m j t")
-            copy(out=dst, in_=src)
+            copy(out=grouped[:].rearrange("p t c j -> p c t j"),
+                 in_=w2_raw[b][:].rearrange("p j (c t) -> p c t j", t=4)[:, :, 2 * u : 2 * u + 2, :])
             codes = keep.tile([P, 2 * P], U32, name=f"w2_codes{b}{u}", align_bytes=64)
             scales = keep.tile([P, 2 * P], U8, name=f"w2_scales{b}{u}", align_bytes=64)
-            nc.vector.quantize_mx(out=codes[:].bitcast(FP8X4), scales=scales[:], in_=grouped[:].rearrange("p t m j -> p (t m j)"))
+            nc.vector.quantize_mx(out=codes[:].bitcast(FP8X4), scales=scales[:], in_=grouped[:].rearrange("p t c j -> p (t c j)"))
             w2_q[b, u] = (codes, scales)
 
         limited = {}
 
         def limit(n):
-            b, t = divmod(n, 4)
-            codes, scales = w2_q[b, t // 2]
-            cols = slice(P * (t % 2), P * (t % 2 + 1))
-            acc = psum.tile([P, BANK], F32, name="acc_b", tag="acc_by", bufs=4)
+            codes, scales = w2_q[n // 4, n % 4 // 2]
+            cols = slice(P * (n % 2), P * (n % 2 + 1))
+            acc = psum.tile([P, P2], F32, name="acc_b", tag="acc_later")
             nc.tensor.matmul_mx(out=acc[:], lhsT=codes[:, cols].bitcast(FP8X4), lhsT_scale=scales[:, cols],
-                                rhs=v2_w[:].bitcast(FP8X4), rhs_scale=v2_s[:], start=True, stop=True)
-            first = max(start for start in cap_sb if start <= n)
-            limited[n] = ring.tile([P, P2], F32, name="low", tag="low_z", align_bytes=64, bufs=3)
-            nc.vector.tensor_tensor(out=limited[n][:], in0=acc[:], in1=cap_sb[first][:, n - first, :], op=ALU.min)
+                                rhs=v2_w[:].bitcast(FP8X4), rhs_scale=v2_s[V2_SCALE_ROW:, :], start=True, stop=True)
+            limited[n] = ring.tile([P, P2], F32, name="limited", tag="limited_z", align_bytes=64)
+            nc.vector.tensor_tensor(out=limited[n][:], in0=acc[:], in1=cap_sb[n][:], op=ALU.min)
 
         def put(n):
-            first = n % 4 // 2 * 2
-            nc.vector.tensor_tensor(pages[n % 4][:].indirect(p1[:]), limited[n][:], wgs_sb[first][:, n % 4 - first, :], ALU.mult)
+            nc.vector.tensor_tensor(pages[n % 4][:].indirect(p1[:]), limited[n][:], wgs_sb[n % 4][:], ALU.mult)
 
-        def scale_by_place(t):
-            nc.vector.tensor_tensor(out=place_sb[0][:, t, :], in0=pages[t][:], in1=place_sb[0][:, t, :], op=ALU.mult)
-
-        nc.vector.tensor_copy(v2_w[:], tab2_w[:].bitcast(U32).indirect(idx2[:]))
-        nc.vector.tensor_copy(v2_s[:], tab2_s[:].indirect(idx2[:]))
         quantise_w2(0, 0, nc.vector.tensor_copy)
         quantise_w2(0, 1, nc.scalar.copy)
+        nc.vector.tensor_copy(v2_s[:], tab2_s[:].indirect(idx2[:]))
+        nc.vector.tensor_copy(v2_w[:], tab2_w[:].bitcast(U32).indirect(idx2[:]))
+
         w1_dealt = []
         for b in range(2):
-            words = keep.tile([P, 2, 2 * BANK], U8, name=f"w1_dealt_w{b}", align_bytes=64)
-            scales = keep.tile([P, 2, BANK], U8, name=f"w1_dealt_s{b}", align_bytes=64)
-            nc.vector.tensor_copy(out=scales[:].rearrange("p a (t q) -> p a t q", t=4),
-                                  in_=w1_s[:, :, BANK * b : BANK * (b + 1)].rearrange("p a (q t) -> p a t q", t=4))
-            nc.scalar.copy(out=words[:].bitcast(U16).rearrange("p a (t q) -> p a t q", t=4),
-                           in_=w1_w[:].bitcast(U16)[:, :, BANK * b : BANK * (b + 1)].rearrange("p a (q t) -> p a t q", t=4))
+            cols = slice(PASS * b, PASS * (b + 1))
+            words = keep.tile([P, 2, 2 * PASS], U8, name=f"w1_dealt_w{b}", align_bytes=64)
+            scales = keep.tile([P, 2, PASS], U8, name=f"w1_dealt_s{b}", align_bytes=64)
+            nc.vector.tensor_copy(out=scales[:].rearrange("p a (t c) -> p a t c", t=4),
+                                  in_=w1_s[:, :, cols].rearrange("p a (c t) -> p a t c", t=4))
+            nc.scalar.copy(out=words[:].bitcast(U16).rearrange("p a (t c) -> p a t c", t=4),
+                           in_=w1_w[:].bitcast(U16)[:, :, cols].rearrange("p a (c t) -> p a t c", t=4))
             w1_dealt.append((words, scales))
 
         limit(0)
         limit(1)
         put(0)
         put(1)
-        quantise_w2(1, 0, nc.scalar.copy)
-        quantise_w2(1, 1, nc.scalar.copy)
         nc.vector.tensor_copy(v_s[0][:], tab_s[:].indirect(idx[:]))
         for q in range(4):
             nc.scalar.dma_start(out=v_s[1][32 * q : 32 * q + 4, :].bitcast(I32), in_=v_s[0][32 * q + 4 : 32 * q + 8, :].bitcast(I32))
+        limit(2)
+        put(2)
+
         nc.vector.tensor_copy(v_w[0][:], tab_w[0][:].bitcast(U32).indirect(idx[:]))
         for h in range(2):
             nc.vector.tensor_copy(v_w[1][:, HALF * h : HALF * (h + 1)],
                                   tab_w[1][:].bitcast(U32).indirect(idx[:, HALF // 16 * h : HALF // 16 * (h + 1)]))
-        limit(2)
         limit(3)
-        put(2)
-        for n in range(3, 8):
-            if n >= 4:
-                scale_by_place(n - 4)
-            if n + 1 < 8:
-                limit(n + 1)
-            put(n)
+        put(3)
+        quantise_w2(1, 0, nc.vector.tensor_copy)
+        quantise_w2(1, 1, nc.vector.tensor_copy)
+        limit(4)
+        for t in range(4):
+            nc.vector.tensor_tensor(out=place_sb[0][:, t, :], in0=pages[t][:], in1=place_sb[0][:, t, :], op=ALU.mult)
+            if t < 3:
+                limit(5 + t)
+            put(4 + t)
 
         a_sb = {}
 
         def square(h, b, t):
             if t == 0:
-                a_sb[h, b] = shared.tile([P, 4, HALF], F32, name=f"a{h}{b}", offset=A_OFFSETS[2 * h + b])
+                a_sb[h, b] = shared.tile([P, 4, HALF], F32, name=f"a{h}{b}", offset=4 * 4 * HALF * (2 * h + b))
             words, scales = w1_dealt[b]
-            cols = slice(HALF * h, HALF * (h + 1))
-            acc = psum.tile([P, BANK], F32, name="acc_rough", bufs=4)
+            half = slice(HALF * h, HALF * (h + 1))
+            acc = psum.tile([P, HALF], F32, name="acc_rough", tag="acc_first")
             for a in range(2):
                 nc.tensor.matmul_mx(out=acc[:], lhsT=words[:, a, 2 * P * t : 2 * P * (t + 1)].bitcast(FP4X4),
                                     lhsT_scale=scales[:, a, P * t : P * (t + 1)],
-                                    rhs=v_w[a][:, cols].bitcast(FP8X4), rhs_scale=v_s[a][:, cols], start=(a == 0), stop=(a == 1))
+                                    rhs=v_w[a][:, half].bitcast(FP8X4), rhs_scale=v_s[a][:, half], start=(a == 0), stop=(a == 1))
             nc.scalar.activation(out=a_sb[h, b][:, t, :], in_=acc[:], func=ACT.Square)
 
         def root(h, b):
-            whole = a_sb[h, b][:].rearrange("p t c -> p (t c)")
-            nc.scalar.activation(out=whole, in_=whole, func=ACT.Sqrt, bias=1.0)
+            for u in range(2):
+                rows = a_sb[h, b][:, 2 * u : 2 * u + 2, :]
+                nc.scalar.activation(out=rows, in_=rows, func=ACT.Sqrt, bias=1.0)
 
         def apply_gain(h, b, t):
             rows = a_sb[h, b][:, t, :]
             nc.scalar.activation(out=rows, in_=rows, func=ACT.Copy, scale=gain_sb[:, b, t : t + 1])
 
-        units = [(h, b) for h in range(2) for b in range(2)]
-        for before, now in zip([None] + units, units + [None]):
+        a_tiles = [(h, b) for h in range(2) for b in range(2)]
+        for before, now in zip([None] + a_tiles, a_tiles + [None]):
             for t in range(4):
                 if now is not None:
                     square(*now, t)
@@ -225,54 +225,47 @@ def tile_list_hull_drag_features_kernel(tc, tab_words, tab_scales, tab2_words, t
             if now is not None:
                 root(*now)
 
-        z_bf = {}
-        z_q = {}
-
         scaled = {}
+        z_bf = {}
 
-        def scale_chunk(c0, w, t):
+        def scale_chunk(c0, t):
             if t == 0:
-                scaled[c0] = ring.tile([P, 4, w], F32, name="scaled")
-            nc.vector.tensor_tensor(out=scaled[c0][:, t, :], in0=pages[t][:, c0 : c0 + w], in1=place_sb[1][:, t, c0 : c0 + w], op=ALU.mult)
+                scaled[c0] = ring.tile([P, 4, CHUNK], F32, name="scaled")
+            cols = slice(c0, c0 + CHUNK)
+            nc.vector.tensor_tensor(out=scaled[c0][:, t, :], in0=pages[t][:, cols], in1=place_sb[1][:, t, cols], op=ALU.mult)
 
-        def add_up(c0, w):
-            h, local = c0 // HALF, slice(c0 % HALF, c0 % HALF + w)
-            z_bf[c0] = ring.tile([P, 2, w, 4], BF16, name="z_bf", tag="low_z", align_bytes=64, bufs=3)
-            for b, placed in enumerate((place_sb[0][:, :, c0 : c0 + w], scaled[c0][:])):
+        def add_up(c0):
+            h, local = c0 // HALF, slice(c0 % HALF, c0 % HALF + CHUNK)
+            z_bf[c0] = ring.tile([P, 2, CHUNK, 4], BF16, name="z_bf", tag="limited_z", align_bytes=64)
+            for b, product in enumerate((place_sb[0][:, :, c0 : c0 + CHUNK], scaled[c0][:])):
                 nc.vector.tensor_tensor(out=z_bf[c0][:, b].rearrange("p (c i) t -> p c t i", i=RUN),
                                         in0=a_sb[h, b][:, :, local].rearrange("p t (c i) -> p c t i", i=RUN),
-                                        in1=placed.rearrange("p t (c i) -> p c t i", i=RUN), op=ALU.add)
+                                        in1=product.rearrange("p t (c i) -> p c t i", i=RUN), op=ALU.add)
 
-        def quantise_z(c0, w):
-            codes = ring.tile([P, 2 * w], U32, name="z_codes", align_bytes=64, bufs=3)
-            scales = ring.tile([P, 2 * w], U8, name="z_scales", align_bytes=64, bufs=3)
+        def finish(c0, banks):
+            codes = ring.tile([P, 2 * CHUNK], U32, name="z_codes", align_bytes=64, bufs=3)
+            scales = ring.tile([P, 2 * CHUNK], U8, name="z_scales", align_bytes=64, bufs=3)
             nc.vector.quantize_mx(out=codes[:].bitcast(FP8X4), scales=scales[:], in_=z_bf[c0][:].rearrange("p b c t -> p (b c t)"))
-            z_q[c0] = (codes, scales)
-
-        def finish(c0, w, groups):
-            codes, scales = z_q[c0]
-            res = ring.tile([P, len(groups), w], F32, name="res", tag="cap_out", bufs=6)
-            for first in range(0, len(groups), 2 if w == 256 else 4):
-                bank = groups[first : first + BANK // w]
-                acc = psum.tile([P, len(bank), w], F32, name="acc_y", tag="acc_by", bufs=4)
-                for place_in_bank, g in enumerate(bank):
-                    cols = slice(P * g, P * (g + 1))
+            for groups in banks:
+                res = ring.tile([P, len(groups), CHUNK], F32, name="res", tag="cap_out", bufs=8)
+                acc = psum.tile([P, len(groups), CHUNK], F32, name="acc_y", tag="acc_later")
+                for slot, g in enumerate(groups):
+                    rows = slice(P * g, P * (g + 1))
                     for b in range(2):
-                        nc.tensor.matmul_mx(out=acc[:, place_in_bank, :], lhsT=w3_w[:, b, cols].bitcast(FP8X4), lhsT_scale=w3_s[:, b, cols],
-                                            rhs=codes[:, w * b : w * (b + 1)].bitcast(FP8X4), rhs_scale=scales[:, w * b : w * (b + 1)],
-                                            start=(b == 0), stop=(b == 1))
-                nc.scalar.activation(out=res[:, first : first + len(bank), :], in_=acc[:], func=ACT.Abs)
-            nc.scalar.activation(out=res[:], in_=res[:], func=ACT.Ln, bias=1.0)
-            nc.sync.dma_start(out=out.rearrange("(g p) j -> p g j", p=P)[:, groups[0] : groups[-1] + 1, c0 : c0 + w], in_=res[:])
+                        cols = slice(CHUNK * b, CHUNK * (b + 1))
+                        nc.tensor.matmul_mx(out=acc[:, slot, :], lhsT=w3_w[:, b, rows].bitcast(FP8X4), lhsT_scale=w3_s[:, b, rows],
+                                            rhs=codes[:, cols].bitcast(FP8X4), rhs_scale=scales[:, cols], start=(b == 0), stop=(b == 1))
+                nc.scalar.activation(out=res[:], in_=acc[:], func=ACT.Abs)
+                nc.scalar.activation(out=res[:], in_=res[:], func=ACT.Ln, bias=1.0)
+                nc.sync.dma_start(out=out.rearrange("(g p) j -> p g j", p=P)[:, groups[0] : groups[-1] + 1, c0 : c0 + CHUNK], in_=res[:])
 
-        for before, now in zip([None] + CHUNKS, CHUNKS + [None]):
+        chunks = list(range(0, S, CHUNK))
+        for before, now in zip([None] + chunks, chunks + [None]):
             if now is not None:
-                scale_chunk(*now, 0)
+                scale_chunk(now, 0)
             if before is not None:
-                quantise_z(*before)
-                for groups in ([[0, 1, 2, 3]] if now is not None else [[0, 1], [2, 3]]):
-                    finish(*before, groups)
+                finish(before, [[0, 1, 2, 3]] if now is not None else [[0, 1], [2, 3]])
             if now is not None:
                 for t in range(1, 4):
-                    scale_chunk(*now, t)
-                add_up(*now)
+                    scale_chunk(now, t)
+                add_up(now)

from contextlib import ExitStack

import concourse.mybir as mybir
from concourse.masks import make_identity

K, K2, T, T3, S, P2, H, N = 1024, 512, 4096, 2048, 1024, 512, 1024, 512
FLOPS = 2 * (K * H * S + K2 * H * P2 + H * N * S)

F32 = mybir.dt.float32
BF16 = mybir.dt.bfloat16
I32 = mybir.dt.int32
U32 = mybir.dt.uint32
U16 = mybir.dt.uint16
U8 = mybir.dt.uint8
FP8X4 = mybir.dt.float8_e4m3fn_x4
FP4X4 = mybir.dt.float4_e2m1fn_x4
ACT = mybir.ActivationFunctionType
ALU = mybir.AluOpType

P = 128
PASS = 512
HALF = S // 2
CHUNK = 128
RUN = 4
V2_SCALE_ROW = 8


def tile_list_hull_drag_features_kernel(tc, tab_words, tab_scales, tab2_words, tab2_scales, offs, offs2, pos1,
                                                 w1_words, w1_scales, w2, w3_words, w3_scales, gain, cap, wgs, place, out):
    nc = tc.nc
    with ExitStack() as ctx:
        lists = ctx.enter_context(tc.tile_pool(name="lists", bufs=1))
        keep = ctx.enter_context(tc.tile_pool(name="keep", bufs=1))
        shared = ctx.enter_context(tc.tile_pool(name="shared", bufs=1))
        ring = ctx.enter_context(tc.tile_pool(name="ring", bufs=2))
        psum = ctx.enter_context(tc.psum_pool(name="psum", bufs=4))

        idx = lists.tile([P, S // 16], U16, name="idx")
        idx2 = lists.tile([P, P2 // 16], U16, name="idx2")
        p1 = lists.tile([P, P2 // 16], U16, name="p1")

        tab2_w = keep.tile([P, T3], I32, name="tab2_w", align_bytes=64)
        tab2_s = keep.tile([P, T3], U8, name="tab2_s", align_bytes=64)
        tab_s = keep.tile([P, T], U8, name="tab_s", align_bytes=64)
        tab_w = [shared.tile([P, T], I32, name=f"tab_w{a}", offset=4 * T * a) for a in range(2)]
        v2_w = keep.tile([P, P2], U32, name="v2_w", align_bytes=64)
        v2_s = keep.tile([P, P2], U8, name="v2_s", align_bytes=64)
        v_w = [keep.tile([P, S], U32, name=f"v_w{a}", align_bytes=64) for a in range(2)]
        v_s = [keep.tile([P, S], U8, name=f"v_s{a}", align_bytes=64) for a in range(2)]
        w1_w = keep.tile([P, 2, 2 * H], U8, name="w1_w", align_bytes=64)
        w1_s = keep.tile([P, 2, H], U8, name="w1_s", align_bytes=64)
        w3_w = keep.tile([P, 2, N], I32, name="w3_w", align_bytes=64)
        w3_s = keep.tile([P, 2, N], U8, name="w3_s", align_bytes=64)
        w2_raw = [keep.tile([P, 4, PASS], F32, name=f"w2_raw{b}") for b in range(2)]
        gain_sb = keep.tile([P, 2, 4], F32, name="gain_sb")
        wgs_raw = keep.tile([P, P2], F32, name="wgs_raw")
        wgs_turned = keep.tile([P, 4, 4, P], F32, name="wgs_turned")
        wgs_sb = [keep.tile([P, P2], F32, name=f"wgs{t}") for t in range(4)]
        ident = keep.tile([P, P], F32, name="ident")
        cap_sb = [ring.tile([P, P2], F32, name=f"cap{n}", tag="cap_out", bufs=8) for n in range(8)]
        place_sb = [keep.tile([P, 4, S], F32, name=f"place{b}") for b in range(2)]
        pages = [keep.tile([P, S], F32, name=f"page{t}") for t in range(4)]

        nc.gpsimd.memset(tab2_s[:].bitcast(I32), 0)
        make_identity(nc, ident[:])
        for scale_tile in (w1_s, tab_s, w3_s, v_s[1]):
            nc.vector.memset(scale_tile[:].bitcast(I32), 0)
        for page in pages:
            nc.vector.memset(page[:], 0.0)

        def load_weight_scales(scale_tile, dram):
            rows = dram.bitcast(I32).rearrange("a (q r) c -> q r a c", r=4)
            for q in range(4):
                nc.sync.dma_start(out=scale_tile[32 * q : 32 * q + 4].bitcast(I32), in_=rows[q])

        def load_w2(b):
            nc.sync.dma_start(out=w2_raw[b][:], in_=w2.rearrange("(p j) c -> p j c", j=4)[:, :, PASS * b : PASS * (b + 1)])

        def slice_rows(dram, b):
            return dram[PASS * b : PASS * (b + 1), :].rearrange("(p t) j -> p t j", t=4)

        def load_cap(n):
            nc.sync.dma_start(out=cap_sb[n][:], in_=slice_rows(cap, n // 4)[:, n % 4, :])

        def load_tab(a):
            nc.sync.dma_start(out=tab_w[a][:], in_=tab_words[a].rearrange("p t i -> p (t i)").bitcast(I32))

        nc.sync.dma_start(idx2[:], offs2)
        nc.sync.dma_start(out=wgs_raw[:], in_=wgs)
        load_w2(0)
        for q in range(4):
            first_row = 32 * q + V2_SCALE_ROW
            nc.sync.dma_start(out=tab2_s[first_row : first_row + 4, :].bitcast(I32), in_=tab2_scales[0, 4 * q : 4 * q + 4, :].bitcast(I32))
        nc.sync.dma_start(out=tab2_w[:], in_=tab2_words[0].rearrange("p t i -> p (t i)").bitcast(I32))
        load_weight_scales(w1_s, w1_scales)
        load_cap(0)
        nc.sync.dma_start(p1[:], pos1)
        load_cap(1)
        nc.sync.dma_start(idx[:], offs)
        for q in range(4):
            nc.sync.dma_start(out=tab_s[32 * q : 32 * q + 8, :].bitcast(I32), in_=tab_scales[:, 4 * q : 4 * q + 4, :].bitcast(I32))
        load_cap(2)
        load_tab(0)
        nc.sync.dma_start(out=w1_w[:].bitcast(I32), in_=w1_words.bitcast(I32).rearrange("a p c -> p a c"))
        load_tab(1)
        load_cap(3)
        load_w2(1)
        nc.sync.dma_start(out=gain_sb[:], in_=gain.rearrange("(b p t) -> p b t", b=2, t=4))
        for t in range(4):
            nc.sync.dma_start(out=place_sb[0][:, t, :], in_=slice_rows(place, 0)[:, t, :])
            load_cap(4 + t)
        load_weight_scales(w3_s, w3_scales)
        nc.sync.dma_start(out=w3_w[:], in_=w3_words.rearrange("a p c i -> p a (c i)").bitcast(I32))
        for h in range(2):
            half = slice(HALF * h, HALF * (h + 1))
            nc.sync.dma_start(out=place_sb[1][:, :, half], in_=slice_rows(place, 1)[:, :, half])

        turned = psum.tile([P, 4, P], F32, name="wgs_first_turn", tag="acc_first")
        for jt in range(4):
            nc.tensor.transpose(turned[:, jt, :], wgs_raw[:, P * jt : P * (jt + 1)], ident[:])
        for q in range(4):
            nc.scalar.copy(out=wgs_turned[:, :, :, 32 * q : 32 * (q + 1)], in_=turned[:].rearrange("p jt (e t) -> p jt t e", t=4))
        for t in range(4):
            back = psum.tile([P, P2], F32, name="wgs_second_turn", tag="acc_later")
            for jt in range(4):
                nc.tensor.transpose(back[:, P * jt : P * (jt + 1)], wgs_turned[:, jt, t, :], ident[:])
            nc.scalar.copy(out=wgs_sb[t][:], in_=back[:])

        w2_q = {}

        def quantise_w2(b, u, copy):
            grouped = ring.tile([P, 2, P, 4], BF16, name="w2_grouped", align_bytes=64, bufs=4)
            copy(out=grouped[:].rearrange("p t c j -> p c t j"),
                 in_=w2_raw[b][:].rearrange("p j (c t) -> p c t j", t=4)[:, :, 2 * u : 2 * u + 2, :])
            codes = keep.tile([P, 2 * P], U32, name=f"w2_codes{b}{u}", align_bytes=64)
            scales = keep.tile([P, 2 * P], U8, name=f"w2_scales{b}{u}", align_bytes=64)
            nc.vector.quantize_mx(out=codes[:].bitcast(FP8X4), scales=scales[:], in_=grouped[:].rearrange("p t c j -> p (t c j)"))
            w2_q[b, u] = (codes, scales)

        limited = {}

        def limit(n):
            codes, scales = w2_q[n // 4, n % 4 // 2]
            cols = slice(P * (n % 2), P * (n % 2 + 1))
            acc = psum.tile([P, P2], F32, name="acc_b", tag="acc_later")
            nc.tensor.matmul_mx(out=acc[:], lhsT=codes[:, cols].bitcast(FP8X4), lhsT_scale=scales[:, cols],
                                rhs=v2_w[:].bitcast(FP8X4), rhs_scale=v2_s[V2_SCALE_ROW:, :], start=True, stop=True)
            limited[n] = ring.tile([P, P2], F32, name="limited", tag="limited_z", align_bytes=64)
            nc.vector.tensor_tensor(out=limited[n][:], in0=acc[:], in1=cap_sb[n][:], op=ALU.min)

        def put(n):
            nc.vector.tensor_tensor(pages[n % 4][:].indirect(p1[:]), limited[n][:], wgs_sb[n % 4][:], ALU.mult)

        quantise_w2(0, 0, nc.vector.tensor_copy)
        quantise_w2(0, 1, nc.scalar.copy)
        nc.vector.tensor_copy(v2_s[:], tab2_s[:].indirect(idx2[:]))
        nc.vector.tensor_copy(v2_w[:], tab2_w[:].bitcast(U32).indirect(idx2[:]))

        w1_dealt = []
        for b in range(2):
            cols = slice(PASS * b, PASS * (b + 1))
            words = keep.tile([P, 2, 2 * PASS], U8, name=f"w1_dealt_w{b}", align_bytes=64)
            scales = keep.tile([P, 2, PASS], U8, name=f"w1_dealt_s{b}", align_bytes=64)
            nc.vector.tensor_copy(out=scales[:].rearrange("p a (t c) -> p a t c", t=4),
                                  in_=w1_s[:, :, cols].rearrange("p a (c t) -> p a t c", t=4))
            nc.scalar.copy(out=words[:].bitcast(U16).rearrange("p a (t c) -> p a t c", t=4),
                           in_=w1_w[:].bitcast(U16)[:, :, cols].rearrange("p a (c t) -> p a t c", t=4))
            w1_dealt.append((words, scales))

        limit(0)
        limit(1)
        put(0)
        put(1)
        nc.vector.tensor_copy(v_s[0][:], tab_s[:].indirect(idx[:]))
        for q in range(4):
            nc.scalar.dma_start(out=v_s[1][32 * q : 32 * q + 4, :].bitcast(I32), in_=v_s[0][32 * q + 4 : 32 * q + 8, :].bitcast(I32))
        limit(2)
        put(2)

        nc.vector.tensor_copy(v_w[0][:], tab_w[0][:].bitcast(U32).indirect(idx[:]))
        for h in range(2):
            nc.vector.tensor_copy(v_w[1][:, HALF * h : HALF * (h + 1)],
                                  tab_w[1][:].bitcast(U32).indirect(idx[:, HALF // 16 * h : HALF // 16 * (h + 1)]))
        limit(3)
        put(3)
        quantise_w2(1, 0, nc.vector.tensor_copy)
        quantise_w2(1, 1, nc.vector.tensor_copy)
        limit(4)
        for t in range(4):
            nc.vector.tensor_tensor(out=place_sb[0][:, t, :], in0=pages[t][:], in1=place_sb[0][:, t, :], op=ALU.mult)
            if t < 3:
                limit(5 + t)
            put(4 + t)

        a_sb = {}

        def square(h, b, t):
            if t == 0:
                a_sb[h, b] = shared.tile([P, 4, HALF], F32, name=f"a{h}{b}", offset=4 * 4 * HALF * (2 * h + b))
            words, scales = w1_dealt[b]
            half = slice(HALF * h, HALF * (h + 1))
            acc = psum.tile([P, HALF], F32, name="acc_rough", tag="acc_first")
            for a in range(2):
                nc.tensor.matmul_mx(out=acc[:], lhsT=words[:, a, 2 * P * t : 2 * P * (t + 1)].bitcast(FP4X4),
                                    lhsT_scale=scales[:, a, P * t : P * (t + 1)],
                                    rhs=v_w[a][:, half].bitcast(FP8X4), rhs_scale=v_s[a][:, half], start=(a == 0), stop=(a == 1))
            nc.scalar.activation(out=a_sb[h, b][:, t, :], in_=acc[:], func=ACT.Square)

        def root(h, b):
            for u in range(2):
                rows = a_sb[h, b][:, 2 * u : 2 * u + 2, :]
                nc.scalar.activation(out=rows, in_=rows, func=ACT.Sqrt, bias=1.0)

        def apply_gain(h, b, t):
            rows = a_sb[h, b][:, t, :]
            nc.scalar.activation(out=rows, in_=rows, func=ACT.Copy, scale=gain_sb[:, b, t : t + 1])

        a_tiles = [(h, b) for h in range(2) for b in range(2)]
        for before, now in zip([None] + a_tiles, a_tiles + [None]):
            for t in range(4):
                if now is not None:
                    square(*now, t)
                if before is not None:
                    apply_gain(*before, t)
            if now is not None:
                root(*now)

        scaled = {}
        z_bf = {}

        def scale_chunk(c0, t):
            if t == 0:
                scaled[c0] = ring.tile([P, 4, CHUNK], F32, name="scaled")
            cols = slice(c0, c0 + CHUNK)
            nc.vector.tensor_tensor(out=scaled[c0][:, t, :], in0=pages[t][:, cols], in1=place_sb[1][:, t, cols], op=ALU.mult)

        def add_up(c0):
            h, local = c0 // HALF, slice(c0 % HALF, c0 % HALF + CHUNK)
            z_bf[c0] = ring.tile([P, 2, CHUNK, 4], BF16, name="z_bf", tag="limited_z", align_bytes=64)
            for b, product in enumerate((place_sb[0][:, :, c0 : c0 + CHUNK], scaled[c0][:])):
                nc.vector.tensor_tensor(out=z_bf[c0][:, b].rearrange("p (c i) t -> p c t i", i=RUN),
                                        in0=a_sb[h, b][:, :, local].rearrange("p t (c i) -> p c t i", i=RUN),
                                        in1=product.rearrange("p t (c i) -> p c t i", i=RUN), op=ALU.add)

        def finish(c0, banks):
            codes = ring.tile([P, 2 * CHUNK], U32, name="z_codes", align_bytes=64, bufs=3)
            scales = ring.tile([P, 2 * CHUNK], U8, name="z_scales", align_bytes=64, bufs=3)
            nc.vector.quantize_mx(out=codes[:].bitcast(FP8X4), scales=scales[:], in_=z_bf[c0][:].rearrange("p b c t -> p (b c t)"))
            for groups in banks:
                res = ring.tile([P, len(groups), CHUNK], F32, name="res", tag="cap_out", bufs=8)
                acc = psum.tile([P, len(groups), CHUNK], F32, name="acc_y", tag="acc_later")
                for slot, g in enumerate(groups):
                    rows = slice(P * g, P * (g + 1))
                    for b in range(2):
                        cols = slice(CHUNK * b, CHUNK * (b + 1))
                        nc.tensor.matmul_mx(out=acc[:, slot, :], lhsT=w3_w[:, b, rows].bitcast(FP8X4), lhsT_scale=w3_s[:, b, rows],
                                            rhs=codes[:, cols].bitcast(FP8X4), rhs_scale=scales[:, cols], start=(b == 0), stop=(b == 1))
                nc.scalar.activation(out=res[:], in_=acc[:], func=ACT.Abs)
                nc.scalar.activation(out=res[:], in_=res[:], func=ACT.Ln, bias=1.0)
                nc.sync.dma_start(out=out.rearrange("(g p) j -> p g j", p=P)[:, groups[0] : groups[-1] + 1, c0 : c0 + CHUNK], in_=res[:])

        chunks = list(range(0, S, CHUNK))
        for before, now in zip([None] + chunks, chunks + [None]):
            if now is not None:
                scale_chunk(now, 0)
            if before is not None:
                finish(before, [[0, 1, 2, 3]] if now is not None else [[0, 1], [2, 3]])
            if now is not None:
                for t in range(1, 4):
                    scale_chunk(now, t)
                add_up(now)
